import numpy as np, ml_dtypes
CORES = [1,3,5,9,11,13]
N = 6
import mx_ref
NC = 192
A = np.float32(0.03)
BF = ml_dtypes.bfloat16
def setup_inputs(rng):
    def f(*shape):
        return mx_ref.flush((rng.standard_normal(shape, dtype=np.float32) * np.exp2(rng.integers(-2, 3, shape[:-1] + (1,)))).astype(BF))
    tg = np.stack([rng.integers(0, N, (N, 128)), rng.integers(0, NC, (N, 128))], axis=2).astype(BF)
    return {"tg": tg, "x": f(N, 128, 512), "w": f(N, 128, 4 * NC)}
def setup_inputs_blocks(rng):
    d = setup_inputs(rng)
    for k in ("x", "w"): d[k] = mx_ref.spread(d[k], rng, 2)
    return d
def setup_inputs_sharp(rng):
    d = setup_inputs(rng); d["w"] = (d["w"].astype(np.float32) * 32).astype(BF)
    return d
def setup_inputs_apart(rng):
    d = setup_inputs(rng); d["w"] = mx_ref.flush((d["w"].astype(np.float32) * np.exp2(rng.permutation(np.linspace(-3, 3, N))).astype(np.float32).reshape(N, 1, 1)).astype(BF))
    return d
def reference(tg, x, w):
    W = [mx_ref.quantize(w[r]) for r in range(N)]
    y = np.zeros((N, 128, 2), np.float32)
    for j in range(N):
        X = mx_ref.quantize(x[j])
        L = [(mx_ref.matmul(X, W[r]) * A).astype(np.float64) for r in range(N)]
        m = np.max([l.max(axis=1, keepdims=True) for l in L], axis=0); s = sum(np.exp(l - m).sum(axis=1, keepdims=True) for l in L)
        t = np.array([[L[int(a) % N][i, int(c) % NC]] for i, (a, c) in enumerate(tg[j].astype(np.float32))])
        y[j] = np.concatenate([np.log(s) + m - t, np.log(s) + m], axis=1).astype(np.float32)
    return {"y": y}

@@ -1,0 +1,300 @@
+import numpy as np
+from concourse.bass import DstId, RemoteDMATransfer
+from concourse.mybir import dt, AluOpType as OP, AxisListType, ActivationFunctionType as AF
+
+SIM_CORES = 16
+NC = 192
+NW = 3 * NC
+H = NW // 2
+SCALE = float(np.float32(0.03))
+GRID = 256.0
+MAGIC = 1.5 * 2.0 ** 23 * GRID
+STEP = SCALE * GRID
+KSTEP = float(np.exp(-STEP))
+LEVELS = 4
+
+NK = 90
+SCRATCH = {
+    "xb": ("sbuf", [128, 512], "bfloat16"),
+    "wb": ("sbuf", [128, 768], "bfloat16"),
+    "tgb": ("sbuf", [128, 16], "bfloat16"),
+    "xq": ("sbuf", [128, 128], "float8_e4m3fn_x4"),
+    "xs": ("sbuf", [128, 128], "uint8"),
+    "wq": ("sbuf", [128, NW], "float8_e4m3fn_x4"),
+    "ws": ("sbuf", [128, NW], "uint8"),
+    "f1q": ("sbuf", [128, 128], "float8_e4m3fn_x4"),
+    "f1s": ("sbuf", [128, 128], "uint8"),
+    "f2q": ("sbuf", [128, 128], "float8_e4m3fn_x4"),
+    "f2s": ("sbuf", [128, 128], "uint8"),
+    "tg1": ("sbuf", [128, 16], "bfloat16"),
+    "tg2": ("sbuf", [128, 16], "bfloat16"),
+    "ra": ("sbuf", [128, 8], "float32"),
+    "rb": ("sbuf", [128, 8], "float32"),
+    "cid": ("sbuf", [128, NW], "float32"),
+    "oa": ("sbuf", [128, 8], "float32"),
+    "ob": ("sbuf", [128, 8], "float32"),
+    "kc": ("sbuf", [128, 8], "float32"),
+    "kl": ("sbuf", [128, 8], "float32"),
+    "wt": ("sbuf", [128, 8], "float32"),
+    "tha": ("sbuf", [128, 8], "float32"),
+    "thb": ("sbuf", [128, 8], "float32"),
+    "hh": ("sbuf", [128, 8], "float32"),
+    "pp": ("sbuf", [128, 8], "float32"),
+    "sc": ("sbuf", [128, 8], "float32"),
+    "bz": ("sbuf", [128, 8], "float32"),
+    "bs": ("sbuf", [128, 8], "float32"),
+    "ln": ("sbuf", [128, 8], "float32"),
+    "yt": ("sbuf", [128, 8], "float32"),
+    "ps": ("psum", [128, 2048], "float32"),
+}
+for _k in (1, 2):
+    SCRATCH["ix%d" % _k] = ("sbuf", [128, 8], "float32")
+    SCRATCH["mk%d" % _k] = ("sbuf", [128, NW], "float32")
+    SCRATCH["pr%d" % _k] = ("sbuf", [128, NW], "float32")
+    SCRATCH["ex%d" % _k] = ("sbuf", [128, NW], "float32")
+    SCRATCH["dm%d" % _k] = ("sbuf", [128, NW], "float32")
+    SCRATCH["mx%d" % _k] = ("sbuf", [128, 8], "float32")
+    SCRATCH["qq%d" % _k] = ("sbuf", [128, 8], "float32")
+    SCRATCH["nb%d" % _k] = ("sbuf", [128, 8], "float32")
+    SCRATCH["sa%d" % _k] = ("sbuf", [128, 8], "float32")
+    SCRATCH["ta%d" % _k] = ("sbuf", [128, 8], "float32")
+    SCRATCH["st%d" % _k] = ("sbuf", [128, 8], "float32")
+SEMAPHORES = ["tg1", "tg2", "f1c", "f1s", "f2c", "f2s", "aw", "ra", "rb", "ls"] + ["k%d" % i for i in range(NK)]
+
+
+def plan(T, topo):
+    chips = sorted({topo.chip(c) for c in T.cores})
+    out = {}
+    for ch in chips:
+        here = [c for c in T.cores if topo.chip(c) == ch]
+        there = [c for c in T.cores if topo.chip(c) != ch]
+        P = [c for c in here if all(topo.may_write(c, d) for d in there)][0]
+        A, B = sorted([c for c in here if c != P], key=lambda c: topo.die(c) != topo.die(P))
+        helpers = [c for c in range(SIM_CORES) if topo.chip(c) == ch and T.rank_of(c) is None and all(topo.may_write(c, d) for d in there)]
+        RA = sorted(helpers, key=lambda c: topo.die(c) != topo.die(A))[0]
+        RB = sorted([c for c in helpers if c != RA], key=lambda c: topo.die(c) != topo.die(B))[0]
+        out[ch] = {"P": P, "A": A, "B": B, "RA": RA, "RB": RB, "base": min(T.rank_of(c) for c in here), "here": here}
+    return chips, out
+
+
+def rank_program(g, core, T, topo):
+    chips, plans = plan(T, topo)
+    ch = topo.chip(core)
+    me = plans[ch]
+    ot = plans[[c for c in chips if c != ch][0]]
+    role = [r for r in ("P", "A", "B", "RA", "RB") if me[r] == core]
+    if not role:
+        return
+    role = role[0]
+    Q = {"g": g, "v": g.vector, "t": g.tensor, "s": g.scalar, "y": g.sync}
+    seen, made, sent = set(), [], [0]
+
+    def need(q, *keys):
+        for k in keys:
+            if (q, k) not in seen:
+                seen.add((q, k))
+                Q[q].wait_ge(T.sem[k[0]], k[1])
+
+    def done(inst, n=1):
+        key = ("k%d" % len(made), n)
+        made.append(key)
+        inst.then_inc(T.sem[key[0]], n)
+        return key
+
+    def engines(dst, lo, n):
+        m = topo.mask(core, dst)
+        bits = [i for i in range(m.bit_length()) if (m >> i) & 1]
+        return sum(1 << i for i in bits[lo:lo + n])
+
+    def count(mask):
+        return bin(mask).count("1")
+
+    def did(c):
+        a = topo.addr(c)
+        return DstId(rid=a[0], pnc=a[1])
+
+    def send(dst, out, in_, sem, mask):
+        a = topo.addr(dst)
+        g.remote_dma(out, in_, T.sem[sem], T.sem.ls, a[1], a[0], mask)
+        sent[0] += count(mask)
+
+    def fused(items):
+        trs = []
+        for dsts, out, in_, sem, mask in items:
+            trs.append(RemoteDMATransfer(dst_ids=[did(d) for d in dsts], dma_engine_mask=mask, remote_sem=T.sem[sem],
+                                         srcs=[in_], dsts=[out for _ in dsts]))
+            sent[0] += count(mask)
+        g.remote_dma_fused(trs, local_sem=T.sem.ls)
+
+    def u8(v):
+        return v.bitcast(dt.uint8)
+
+    NX = 8
+    ND = 8
+    NWE = 16
+    NS = 8
+
+    if role in ("RA", "RB"):
+        dst = ot["P"]
+        k = "1" if role == "RA" else "2"
+        m = engines(dst, 0, NX)
+        need("g", ("tg1", NX))
+        send(dst, T["tg" + k][:, 0:2], T.tg1[:, 0:2], "tg" + k, m)
+        need("g", ("f1c", NX))
+        send(dst, u8(T["f%sq" % k][:, :]), u8(T.f1q[:, :]), "f%sc" % k, m)
+        need("g", ("f1s", NX))
+        send(dst, T["f%ss" % k][:, :], T.f1s[:, :], "f%ss" % k, m)
+        if role == "RA":
+            need("g", ("ra", NS))
+            send(ot["P"] if False else me["P"], T.rb[:, 0:3], T.ra[:, 0:3], "rb", engines(me["P"], 0, NS)) if False else send(dst, T.rb[:, 0:3], T.ra[:, 0:3], "rb", engines(dst, 0, NS))
+        need("g", ("ls", sent[0]))
+        return
+
+    v, s, t, y = g.vector, g.scalar, g.tensor, g.sync
+    slot = (T.rank_of(core) - me["base"]) * NC
+    wq = T.wq[:, slot:slot + NC]
+    ws = T.ws[:, slot:slot + NC]
+
+    kx = done(y.dma_start(T.xb[:, :], T.x[:, :]), 16)
+    ktg = done(s.dma_start(T.tgb[:, 0:2], T.tg[:, :]), 16)
+    kw = done(y.dma_start(T.wb[:, :], T.w[:, :]), 16)
+
+    kio = done(g.iota(T.cid[:, :], [[1, NW]], me["base"] * NC, 0, allow_small_or_imprecise_dtypes=True))
+    G = int(GRID)
+    koa = done(g.iota(T.oa[:, 0:LEVELS], [[G, LEVELS]], -G * (LEVELS - 1), 0, allow_small_or_imprecise_dtypes=True))
+    kob = done(g.iota(T.ob[:, 0:LEVELS], [[-G, LEVELS]], G * (LEVELS - 1), 0, allow_small_or_imprecise_dtypes=True))
+    k0 = done(v.memset(T.kc[:, 0:1], -STEP - float(np.log(1.0 - KSTEP))))
+    k1 = done(v.memset(T.kc[:, 1:LEVELS - 1], -STEP))
+    k2 = done(v.memset(T.kl[:, 0:1], 32.0 * (1.0 - KSTEP)))
+    k3 = done(v.memset(T.wt[:, :], 1.0))
+    need("v", k3)
+    k4 = done(v.memset(T.wt[:, 0:1], 0.0))
+    need("s", k0, k1, k3)
+    kwt = done(s.activation(T.wt[:, 2:2 * LEVELS:2], T.kc[:, 0:LEVELS - 1], AF.Exp))
+
+    need("v", kx)
+    kqx = done(v.quantize_mx(T.xq[:, :], T.xs[:, :], T.xb[:, :]))
+    need("v", kw)
+    kqw = done(v.quantize_mx(wq, ws, T.wb[:, :]))
+
+    mates3 = [c for c in me["here"] if c != core]
+    if role == "P":
+        A2, B1 = ot["A"], me["B"]
+        m1, m2 = engines(A2, 0, NX), engines(B1, NX, ND)
+        need("g", ktg)
+        fused([([A2], T.tg1[:, 0:2], T.tgb[:, 0:2], "tg1", m1), ([B1], T.tg1[:, 0:2], T.tgb[:, 0:2], "tg1", m2)])
+        need("g", kqx)
+        fused([([A2], u8(T.f1q[:, :]), u8(T.xq[:, :]), "f1c", m1), ([B1], u8(T.f1q[:, :]), u8(T.xq[:, :]), "f1c", m2)])
+        fused([([A2], T.f1s[:, :], T.xs[:, :], "f1s", m1), ([B1], T.f1s[:, :], T.xs[:, :], "f1s", m2)])
+    else:
+        R = me["R" + role]
+        m1 = engines(R, 0, NX)
+        need("g", ktg)
+        send(R, T.tg1[:, 0:2], T.tgb[:, 0:2], "tg1", m1)
+        need("g", kqx)
+        send(R, u8(T.f1q[:, :]), u8(T.xq[:, :]), "f1c", m1)
+        send(R, T.f1s[:, :], T.xs[:, :], "f1s", m1)
+    mw = engines(mates3[0], 0, NWE)
+    need("g", kqw)
+    fused([(mates3, u8(wq), u8(wq), "aw", mw)])
+    fused([(mates3, ws, ws, "aw", mw)])
+    kaw = ("aw", 2 * 2 * NWE)
+
+    n1 = ND if role == "B" else NX
+    set1 = (T.f1q, T.f1s, [("f1c", n1), ("f1s", n1)], T.tg1, [("tg1", n1)])
+    if role == "P":
+        set2 = (T.f2q, T.f2s, [("f2c", NX), ("f2s", NX)], T.tg2, [("tg2", NX)])
+    else:
+        set2 = (T.xq, T.xs, [kqx], T.tgb, [ktg])
+    sets = {1: set1, 2: set2}
+
+    kmk = {}
+    for k in ((1, 2) if role == "P" else (2, 1)):
+        tg, kt = sets[k][3], sets[k][4]
+        need("v", *kt)
+        ki = done(v.tensor_scalar(T["ix%d" % k][:, 0:1], tg[:, 0:1], float(NC), tg[:, 1:2], OP.mult, OP.add))
+        need("v", ki, kio)
+        kmk[k] = done(v.tensor_scalar(T["mk%d" % k][:, :], T.cid[:, :], T["ix%d" % k][:, 0:1], SCALE, OP.is_equal, OP.mult))
+
+    kst = {}
+    for k in (1, 2):
+        xq, xs, kxa = sets[k][0], sets[k][1], sets[k][2]
+        b0 = 1024 * (k - 1)
+        pa, pb = T.ps[:, b0:b0 + H], T.ps[:, b0 + 512:b0 + 512 + H]
+        need("t", kqw, kaw, *kxa)
+        kma = done(t.matmul_mx(pa, xq[:, :], xs[:, :], T.wq[:, 0:H], T.ws[:, 0:H], True, True))
+        kmb = done(t.matmul_mx(pb, xq[:, :], xs[:, :], T.wq[:, H:NW], T.ws[:, H:NW], True, True))
+        n = "%d" % k
+        mx, qq, nb, sa, ta, st = T["mx" + n], T["qq" + n], T["nb" + n], T["sa" + n], T["ta" + n], T["st" + n]
+        pr, mk, ex, dm = T["pr" + n], T["mk" + n], T["ex" + n], T["dm" + n]
+        need("v", kma)
+        kxa_ = done(v.tensor_reduce(mx[:, 0:1], pa, AxisListType.X, OP.max))
+        need("v", kmb)
+        kxb_ = done(v.tensor_reduce(mx[:, 1:2], pb, AxisListType.X, OP.max))
+        need("v", kxa_, kxb_)
+        kq = done(v.tensor_scalar(qq[:, 0:1], mx[:, 0:1], mx[:, 1:2], MAGIC, OP.max, OP.add))
+        need("v", kq)
+        knb = done(v.tensor_scalar(nb[:, 0:1], qq[:, 0:1], MAGIC, -SCALE, OP.subtract, OP.mult))
+        need("s", knb)
+        kea = done(s.activation(ex[:, 0:H], pa, AF.Exp, bias=nb[:, 0:1], scale=SCALE, accum_out=sa[:, 0:1]))
+        need("v", kmk[k])
+        kpb = done(v.tensor_tensor(pr[:, H:NW], pb, mk[:, H:NW], OP.mult))
+        need("s", kpb)
+        keb = done(s.activation(ex[:, H:NW], pb, AF.Exp, bias=nb[:, 0:1], scale=SCALE, accum_out=sa[:, 1:2]))
+        kc_ = done(v.tensor_scalar(st[:, 0:1], qq[:, 0:1], MAGIC, None, OP.subtract))
+        need("v", kea)
+        kpa = done(v.tensor_tensor(pr[:, 0:H], pa, mk[:, 0:H], OP.mult))
+        if k == 1:
+            need("s", kpa)
+            kt_ = done(s.activation(dm[:, :], pr[:, :], AF.Identity, accum_out=st[:, 2:3]))
+            need("v", keb)
+            ks_ = done(v.tensor_tensor(st[:, 1:2], sa[:, 0:1], sa[:, 1:2], OP.add))
+        else:
+            need("s", kpa)
+            kta = done(s.activation(dm[:, 0:H], pr[:, 0:H], AF.Identity, accum_out=ta[:, 0:1]))
+            need("v", keb)
+            ks_ = done(v.tensor_tensor(st[:, 1:2], sa[:, 0:1], sa[:, 1:2], OP.add))
+            ktb = done(v.tensor_reduce(ta[:, 1:2], pr[:, H:NW], AxisListType.X, OP.add))
+            need("v", kta, ktb)
+            kt_ = done(v.tensor_tensor(st[:, 2:3], ta[:, 0:1], ta[:, 1:2], OP.add))
+        kst[k] = [kc_, ks_, kt_]
+        if k == 1:
+            dst = {"P": ot["A"], "A": me["RA"], "B": me["P"]}[role]
+            need("g", *kst[1])
+            send(dst, T["rb" if role == "P" else "ra"][:, 0:3], T.st1[:, 0:3], "rb" if role == "P" else "ra", engines(dst, 0, NS))
+        elif role == "P":
+            need("g", *kst[2])
+            send(ot["B"], T.rb[:, 0:3], T.st2[:, 0:3], "rb", engines(ot["B"], 0, NS))
+
+    need("s", k2)
+    kl = done(s.activation(T.hh[:, 1:2], T.kl[:, 0:1], AF.Ln))
+    if role == "P":
+        E, ke = T.ra, [("ra", NS)]
+    else:
+        E, ke = T.st2, kst[2]
+    need("v", koa, kob, *ke)
+    kta_ = done(v.tensor_scalar(T.tha[:, 0:LEVELS], T.oa[:, 0:LEVELS], E[:, 0:1], None, OP.add))
+    ktb_ = done(v.tensor_scalar(T.thb[:, 0:LEVELS], T.ob[:, 0:LEVELS], E[:, 0:1], None, OP.add))
+    need("v", kl)
+    kh = done(v.tensor_tensor(T.hh[:, 0:1], T.hh[:, 1:2], E[:, 2:3], OP.subtract))
+    need("v", kta_, ktb_, kh, kwt, k4, ("rb", NS))
+    F = T.rb
+    kp = done(v.tensor_scalar(T.pp[:, 0:2 * LEVELS:2], T.tha[:, 0:LEVELS], F[:, 0:1], F[:, 1:2], OP.is_le, OP.mult))
+    kr = done(v.tensor_scalar(T.pp[:, 1:2 * LEVELS:2], T.thb[:, 0:LEVELS], F[:, 0:1], E[:, 1:2], OP.is_ge, OP.mult))
+    need("v", kp, kr)
+    ksc = done(v.tensor_tensor_scan(T.sc[:, :], T.wt[:, :], T.pp[:, :], 0.0, OP.mult, OP.add))
+    need("s", ksc)
+    kln = done(s.activation(T.ln[:, 0:1], T.sc[:, 2 * LEVELS - 1:2 * LEVELS], AF.Ln, scale=1.0 / 32.0))
+    kz = done(v.tensor_scalar(T.bz[:, 0:1], F[:, 0:1], E[:, 0:1], SCALE, OP.max, OP.mult))
+    need("v", kz)
+    kb0 = done(v.tensor_scalar(T.bs[:, 0:1], T.bz[:, 0:1], T.hh[:, 0:1], F[:, 2:3], OP.add, OP.subtract))
+    kb1 = done(v.tensor_scalar(T.bs[:, 1:2], T.bz[:, 0:1], T.hh[:, 1:2], None, OP.add))
+    need("v", kb0, kb1, kln)
+    ky = done(v.tensor_scalar(T.yt[:, 0:2], T.bs[:, 0:2], T.ln[:, 0:1], None, OP.add))
+    need("y", ky)
+    kyo = done(y.dma_start(T.y[:, :], T.yt[:, 0:2]), 16)
+    need("y", kyo)
+
+    need("g", ("ls", sent[0]))
+    waited = {k for _, k in seen}
+    need("g", *[k for k in made if k not in waited])

@@ -11,55 +11,39 @@ GRID = 256.0
 MAGIC = 1.5 * 2.0 ** 23 * GRID
 STEP = SCALE * GRID
 KSTEP = float(np.exp(-STEP))
-LEVELS = 4
+LV = 4
 
-NK = 90
+NX1 = 8
+NX = 8
+ND = 8
+NWE = 16
+NS = 16
+
+NK = 110
 SCRATCH = {
     "xb": ("sbuf", [128, 512], "bfloat16"),
     "wb": ("sbuf", [128, 768], "bfloat16"),
-    "tgb": ("sbuf", [128, 16], "bfloat16"),
     "xq": ("sbuf", [128, 128], "float8_e4m3fn_x4"),
     "xs": ("sbuf", [128, 128], "uint8"),
     "wq": ("sbuf", [128, NW], "float8_e4m3fn_x4"),
     "ws": ("sbuf", [128, NW], "uint8"),
-    "f1q": ("sbuf", [128, 128], "float8_e4m3fn_x4"),
-    "f1s": ("sbuf", [128, 128], "uint8"),
-    "f2q": ("sbuf", [128, 128], "float8_e4m3fn_x4"),
-    "f2s": ("sbuf", [128, 128], "uint8"),
-    "tg1": ("sbuf", [128, 16], "bfloat16"),
-    "tg2": ("sbuf", [128, 16], "bfloat16"),
-    "ra": ("sbuf", [128, 8], "float32"),
-    "rb": ("sbuf", [128, 8], "float32"),
     "cid": ("sbuf", [128, NW], "float32"),
-    "oa": ("sbuf", [128, 8], "float32"),
-    "ob": ("sbuf", [128, 8], "float32"),
-    "kc": ("sbuf", [128, 8], "float32"),
-    "kl": ("sbuf", [128, 8], "float32"),
-    "wt": ("sbuf", [128, 8], "float32"),
-    "tha": ("sbuf", [128, 8], "float32"),
-    "thb": ("sbuf", [128, 8], "float32"),
-    "hh": ("sbuf", [128, 8], "float32"),
-    "pp": ("sbuf", [128, 8], "float32"),
-    "sc": ("sbuf", [128, 8], "float32"),
-    "bz": ("sbuf", [128, 8], "float32"),
-    "bs": ("sbuf", [128, 8], "float32"),
-    "ln": ("sbuf", [128, 8], "float32"),
-    "yt": ("sbuf", [128, 8], "float32"),
     "ps": ("psum", [128, 2048], "float32"),
 }
-for _k in (1, 2):
-    SCRATCH["ix%d" % _k] = ("sbuf", [128, 8], "float32")
-    SCRATCH["mk%d" % _k] = ("sbuf", [128, NW], "float32")
-    SCRATCH["pr%d" % _k] = ("sbuf", [128, NW], "float32")
-    SCRATCH["ex%d" % _k] = ("sbuf", [128, NW], "float32")
-    SCRATCH["dm%d" % _k] = ("sbuf", [128, NW], "float32")
-    SCRATCH["mx%d" % _k] = ("sbuf", [128, 8], "float32")
-    SCRATCH["qq%d" % _k] = ("sbuf", [128, 8], "float32")
-    SCRATCH["nb%d" % _k] = ("sbuf", [128, 8], "float32")
-    SCRATCH["sa%d" % _k] = ("sbuf", [128, 8], "float32")
-    SCRATCH["ta%d" % _k] = ("sbuf", [128, 8], "float32")
-    SCRATCH["st%d" % _k] = ("sbuf", [128, 8], "float32")
-SEMAPHORES = ["tg1", "tg2", "f1c", "f1s", "f2c", "f2s", "aw", "ra", "rb", "ls"] + ["k%d" % i for i in range(NK)]
+for _k in ("1", "2"):
+    SCRATCH["f%sq" % _k] = ("sbuf", [128, 128], "float8_e4m3fn_x4")
+    SCRATCH["f%ss" % _k] = ("sbuf", [128, 128], "uint8")
+    for _n in ("mk", "pr", "ex", "dm"):
+        SCRATCH[_n + _k] = ("sbuf", [128, NW], "float32")
+    for _n in ("ix", "mx", "qq", "nb", "sa", "st", "tt"):
+        SCRATCH[_n + _k] = ("sbuf", [128, 8], "float32")
+for _n in ("tgb", "tg1", "tg2"):
+    SCRATCH[_n] = ("sbuf", [128, 16], "bfloat16")
+for _n in ("tgd", "td1"):
+    SCRATCH[_n] = ("dram", [128, 2], "bfloat16")
+for _n in ("ra", "rb", "rt", "oa", "ob", "kc", "kl", "wt", "tha", "thb", "hh", "pp", "sc", "bz", "bs", "ln", "yt"):
+    SCRATCH[_n] = ("sbuf", [128, 8], "float32")
+SEMAPHORES = ["tg1", "tg2", "f1c", "f1s", "f2c", "f2s", "aw", "ra", "rb", "rt", "ls"] + ["k%d" % i for i in range(NK)]
 
 
 def plan(T, topo):
@@ -109,189 +93,269 @@ def rank_program(g, core, T, topo):
     def count(mask):
         return bin(mask).count("1")
 
-    def did(c):
-        a = topo.addr(c)
-        return DstId(rid=a[0], pnc=a[1])
-
     def send(dst, out, in_, sem, mask):
         a = topo.addr(dst)
         g.remote_dma(out, in_, T.sem[sem], T.sem.ls, a[1], a[0], mask)
         sent[0] += count(mask)
 
-    def fused(items):
+    def fused(*items):
         trs = []
         for dsts, out, in_, sem, mask in items:
-            trs.append(RemoteDMATransfer(dst_ids=[did(d) for d in dsts], dma_engine_mask=mask, remote_sem=T.sem[sem],
-                                         srcs=[in_], dsts=[out for _ in dsts]))
+            ids = [DstId(rid=topo.addr(d)[0], pnc=topo.addr(d)[1]) for d in dsts]
+            trs.append(RemoteDMATransfer(dst_ids=ids, dma_engine_mask=mask, remote_sem=T.sem[sem], srcs=[in_], dsts=[out for _ in dsts]))
             sent[0] += count(mask)
         g.remote_dma_fused(trs, local_sem=T.sem.ls)
 
     def u8(v):
         return v.bitcast(dt.uint8)
 
-    NX = 8
-    ND = 8
-    NWE = 16
-    NS = 8
-
     if role in ("RA", "RB"):
         dst = ot["P"]
         k = "1" if role == "RA" else "2"
         m = engines(dst, 0, NX)
-        need("g", ("tg1", NX))
-        send(dst, T["tg" + k][:, 0:2], T.tg1[:, 0:2], "tg" + k, m)
-        need("g", ("f1c", NX))
+        need("g", ("tg1", 1))
+        send(dst, T["tg" + k][:, 0:2], T.td1[:, :], "tg" + k, m)
+        need("g", ("f1c", NX1))
         send(dst, u8(T["f%sq" % k][:, :]), u8(T.f1q[:, :]), "f%sc" % k, m)
-        need("g", ("f1s", NX))
+        need("g", ("f1s", NX1))
         send(dst, T["f%ss" % k][:, :], T.f1s[:, :], "f%ss" % k, m)
         if role == "RA":
             need("g", ("ra", NS))
-            send(ot["P"] if False else me["P"], T.rb[:, 0:3], T.ra[:, 0:3], "rb", engines(me["P"], 0, NS)) if False else send(dst, T.rb[:, 0:3], T.ra[:, 0:3], "rb", engines(dst, 0, NS))
+            send(dst, T.rb[:, 0:2], T.ra[:, 0:2], "rb", m)
+            need("g", ("rt", NS))
+            send(dst, T.rt[:, 0:1], T.rt[:, 0:1], "rt", m)
         need("g", ("ls", sent[0]))
         return
 
     v, s, t, y = g.vector, g.scalar, g.tensor, g.sync
-    slot = (T.rank_of(core) - me["base"]) * NC
+    base = me["base"]
+    slot = (T.rank_of(core) - base) * NC
     wq = T.wq[:, slot:slot + NC]
     ws = T.ws[:, slot:slot + NC]
 
+    ktd = done(s.dma_start(T.tgd[:, :], T.tg[:, :]), 16)
     kx = done(y.dma_start(T.xb[:, :], T.x[:, :]), 16)
-    ktg = done(s.dma_start(T.tgb[:, 0:2], T.tg[:, :]), 16)
     kw = done(y.dma_start(T.wb[:, :], T.w[:, :]), 16)
+    if role != "P":
+        ktg = done(s.dma_start(T.tgb[:, 0:2], T.tg[:, :]), 16)
 
-    kio = done(g.iota(T.cid[:, :], [[1, NW]], me["base"] * NC, 0, allow_small_or_imprecise_dtypes=True))
-    G = int(GRID)
-    koa = done(g.iota(T.oa[:, 0:LEVELS], [[G, LEVELS]], -G * (LEVELS - 1), 0, allow_small_or_imprecise_dtypes=True))
-    kob = done(g.iota(T.ob[:, 0:LEVELS], [[-G, LEVELS]], G * (LEVELS - 1), 0, allow_small_or_imprecise_dtypes=True))
+    kio = [done(g.iota(T.cid[:, 0:NC], [[1, NC]], base * NC, 0, allow_small_or_imprecise_dtypes=True))]
     k0 = done(v.memset(T.kc[:, 0:1], -STEP - float(np.log(1.0 - KSTEP))))
-    k1 = done(v.memset(T.kc[:, 1:LEVELS - 1], -STEP))
+    k1 = done(v.memset(T.kc[:, 1:LV - 1], -STEP))
     k2 = done(v.memset(T.kl[:, 0:1], 32.0 * (1.0 - KSTEP)))
     k3 = done(v.memset(T.wt[:, :], 1.0))
     need("v", k3)
     k4 = done(v.memset(T.wt[:, 0:1], 0.0))
     need("s", k0, k1, k3)
-    kwt = done(s.activation(T.wt[:, 2:2 * LEVELS:2], T.kc[:, 0:LEVELS - 1], AF.Exp))
+    kwt = done(s.activation(T.wt[:, 2:2 * LV:2], T.kc[:, 0:LV - 1], AF.Exp))
+    need("v", kio[0])
+    for j in (1, 2):
+        kio.append(done(v.tensor_scalar(T.cid[:, NC * j:NC * (j + 1)], T.cid[:, 0:NC], float(NC * j), None, OP.add)))
 
     need("v", kx)
     kqx = done(v.quantize_mx(T.xq[:, :], T.xs[:, :], T.xb[:, :]))
     need("v", kw)
     kqw = done(v.quantize_mx(wq, ws, T.wb[:, :]))
 
-    mates3 = [c for c in me["here"] if c != core]
+    others = [c for c in me["here"] if c != core]
+    need("g", ktd)
     if role == "P":
         A2, B1 = ot["A"], me["B"]
         m1, m2 = engines(A2, 0, NX), engines(B1, NX, ND)
-        need("g", ktg)
-        fused([([A2], T.tg1[:, 0:2], T.tgb[:, 0:2], "tg1", m1), ([B1], T.tg1[:, 0:2], T.tgb[:, 0:2], "tg1", m2)])
+        fused(([A2], T.td1[:, :], T.tgd[:, :], "tg1", engines(A2, 0, 1)), ([B1], T.td1[:, :], T.tgd[:, :], "tg1", engines(B1, NX, 1)))
         need("g", kqx)
-        fused([([A2], u8(T.f1q[:, :]), u8(T.xq[:, :]), "f1c", m1), ([B1], u8(T.f1q[:, :]), u8(T.xq[:, :]), "f1c", m2)])
-        fused([([A2], T.f1s[:, :], T.xs[:, :], "f1s", m1), ([B1], T.f1s[:, :], T.xs[:, :], "f1s", m2)])
+        fused(([A2], u8(T.f1q[:, :]), u8(T.xq[:, :]), "f1c", m1), ([B1], u8(T.f1q[:, :]), u8(T.xq[:, :]), "f1c", m2))
+        fused(([A2], T.f1s[:, :], T.xs[:, :], "f1s", m1), ([B1], T.f1s[:, :], T.xs[:, :], "f1s", m2))
     else:
         R = me["R" + role]
-        m1 = engines(R, 0, NX)
-        need("g", ktg)
-        send(R, T.tg1[:, 0:2], T.tgb[:, 0:2], "tg1", m1)
+        m1 = engines(R, 0, NX1)
+        send(R, T.td1[:, :], T.tgd[:, :], "tg1", engines(R, 0, 1))
         need("g", kqx)
         send(R, u8(T.f1q[:, :]), u8(T.xq[:, :]), "f1c", m1)
         send(R, T.f1s[:, :], T.xs[:, :], "f1s", m1)
-    mw = engines(mates3[0], 0, NWE)
+    mw = engines(others[0], 0, NWE)
     need("g", kqw)
-    fused([(mates3, u8(wq), u8(wq), "aw", mw)])
-    fused([(mates3, ws, ws, "aw", mw)])
+    fused((others, u8(wq), u8(wq), "aw", mw))
+    fused((others, ws, ws, "aw", mw))
     kaw = ("aw", 2 * 2 * NWE)
+    G = int(GRID)
+    koa = done(g.iota(T.oa[:, 0:LV], [[G, LV]], -G * (LV - 1), 0, allow_small_or_imprecise_dtypes=True))
+    kob = done(g.iota(T.ob[:, 0:LV], [[-G, LV]], G * (LV - 1), 0, allow_small_or_imprecise_dtypes=True))
 
-    n1 = ND if role == "B" else NX
-    set1 = (T.f1q, T.f1s, [("f1c", n1), ("f1s", n1)], T.tg1, [("tg1", n1)])
+    halves = [(0, H), (H, NW)]
     if role == "P":
-        set2 = (T.f2q, T.f2s, [("f2c", NX), ("f2s", NX)], T.tg2, [("tg2", NX)])
+        sets = {k: (T["f%dq" % k], T["f%ds" % k], [kaw, ("f%dc" % k, NX), ("f%ds" % k, NX)], T["tg%d" % k], ("tg%d" % k, NX), halves) for k in (1, 2)}
     else:
-        set2 = (T.xq, T.xs, [kqx], T.tgb, [ktg])
-    sets = {1: set1, 2: set2}
+        n1 = ND if role == "B" else NX
+        need("y", ("tg1", 1))
+        kt1 = done(y.dma_start(T.tg1[:, 0:2], T.td1[:, :]), 16)
+        sets = {1: (T.f1q, T.f1s, [kaw, ("f1c", n1), ("f1s", n1)], T.tg1, kt1, halves),
+                2: (T.xq, T.xs, [kqx], T.tgb, ktg, [(slot, slot + NC), (NC, NW) if slot == 0 else (0, NW - NC)])}
+    D = {1: {}, 2: {}}
 
-    kmk = {}
-    for k in ((1, 2) if role == "P" else (2, 1)):
-        tg, kt = sets[k][3], sets[k][4]
-        need("v", *kt)
-        ki = done(v.tensor_scalar(T["ix%d" % k][:, 0:1], tg[:, 0:1], float(NC), tg[:, 1:2], OP.mult, OP.add))
-        need("v", ki, kio)
-        kmk[k] = done(v.tensor_scalar(T["mk%d" % k][:, :], T.cid[:, :], T["ix%d" % k][:, 0:1], SCALE, OP.is_equal, OP.mult))
+    def bank(k, h):
+        b = 1024 * (k - 1) + 512 * h
+        lo, hi = sets[k][5][h]
+        return T.ps[:, b:b + hi - lo]
 
-    kst = {}
-    for k in (1, 2):
-        xq, xs, kxa = sets[k][0], sets[k][1], sets[k][2]
-        b0 = 1024 * (k - 1)
-        pa, pb = T.ps[:, b0:b0 + H], T.ps[:, b0 + 512:b0 + 512 + H]
-        need("t", kqw, kaw, *kxa)
-        kma = done(t.matmul_mx(pa, xq[:, :], xs[:, :], T.wq[:, 0:H], T.ws[:, 0:H], True, True))
-        kmb = done(t.matmul_mx(pb, xq[:, :], xs[:, :], T.wq[:, H:NW], T.ws[:, H:NW], True, True))
-        n = "%d" % k
-        mx, qq, nb, sa, ta, st = T["mx" + n], T["qq" + n], T["nb" + n], T["sa" + n], T["ta" + n], T["st" + n]
-        pr, mk, ex, dm = T["pr" + n], T["mk" + n], T["ex" + n], T["dm" + n]
-        need("v", kma)
-        kxa_ = done(v.tensor_reduce(mx[:, 0:1], pa, AxisListType.X, OP.max))
-        need("v", kmb)
-        kxb_ = done(v.tensor_reduce(mx[:, 1:2], pb, AxisListType.X, OP.max))
-        need("v", kxa_, kxb_)
+    def cols(k, name, h):
+        lo, hi = sets[k][5][h]
+        return T[name + "%d" % k][:, lo:hi]
+
+    def small(k, name):
+        return T[name + "%d" % k]
+
+    def mask(k):
+        tg, ix = sets[k][3], small(k, "ix")
+        need("v", sets[k][4])
+        ki = done(v.tensor_scalar(ix[:, 0:1], tg[:, 0:1], float(NC), tg[:, 1:2], OP.mult, OP.add))
+        need("v", ki, *kio)
+        D[k]["m"] = done(v.tensor_scalar(small(k, "mk")[:, :], T.cid[:, :], ix[:, 0:1], SCALE, OP.is_equal, OP.mult))
+
+    def product(k, h):
+        need("t", kqw, *sets[k][2])
+        lo, hi = sets[k][5][h]
+        D[k]["mm%d" % h] = done(t.matmul_mx(bank(k, h), sets[k][0][:, :], sets[k][1][:, :], T.wq[:, lo:hi], T.ws[:, lo:hi], True, True))
+
+    def top(k, h):
+        need("v", D[k]["mm%d" % h])
+        D[k]["x%d" % h] = done(v.tensor_reduce(small(k, "mx")[:, h:h + 1], bank(k, h), AxisListType.X, OP.max))
+
+    def shift(k):
+        mx, qq = small(k, "mx"), small(k, "qq")
+        need("v", D[k]["x0"], D[k]["x1"])
         kq = done(v.tensor_scalar(qq[:, 0:1], mx[:, 0:1], mx[:, 1:2], MAGIC, OP.max, OP.add))
         need("v", kq)
-        knb = done(v.tensor_scalar(nb[:, 0:1], qq[:, 0:1], MAGIC, -SCALE, OP.subtract, OP.mult))
-        need("s", knb)
-        kea = done(s.activation(ex[:, 0:H], pa, AF.Exp, bias=nb[:, 0:1], scale=SCALE, accum_out=sa[:, 0:1]))
-        need("v", kmk[k])
-        kpb = done(v.tensor_tensor(pr[:, H:NW], pb, mk[:, H:NW], OP.mult))
-        need("s", kpb)
-        keb = done(s.activation(ex[:, H:NW], pb, AF.Exp, bias=nb[:, 0:1], scale=SCALE, accum_out=sa[:, 1:2]))
-        kc_ = done(v.tensor_scalar(st[:, 0:1], qq[:, 0:1], MAGIC, None, OP.subtract))
-        need("v", kea)
-        kpa = done(v.tensor_tensor(pr[:, 0:H], pa, mk[:, 0:H], OP.mult))
-        if k == 1:
-            need("s", kpa)
-            kt_ = done(s.activation(dm[:, :], pr[:, :], AF.Identity, accum_out=st[:, 2:3]))
-            need("v", keb)
-            ks_ = done(v.tensor_tensor(st[:, 1:2], sa[:, 0:1], sa[:, 1:2], OP.add))
+        D[k]["nb"] = done(v.tensor_scalar(small(k, "nb")[:, 0:1], qq[:, 0:1], MAGIC, -SCALE, OP.subtract, OP.mult))
+
+    def putc(k):
+        D[k]["c"] = done(v.tensor_scalar(small(k, "st")[:, 0:1], small(k, "qq")[:, 0:1], MAGIC, None, OP.subtract))
+
+    def expo(k, h):
+        need("s", D[k]["nb"])
+        D[k]["e%d" % h] = done(s.activation(cols(k, "ex", h), bank(k, h), AF.Exp, bias=small(k, "nb")[:, 0:1], scale=SCALE,
+                                            accum_out=small(k, "sa")[:, h:h + 1]))
+
+    def puts(k):
+        need("v", D[k]["e0"], D[k]["e1"])
+        D[k]["s"] = done(v.tensor_tensor(small(k, "st")[:, 1:2], small(k, "sa")[:, 0:1], small(k, "sa")[:, 1:2], OP.add))
+
+    def pick(k, h):
+        need("v", D[k]["m"])
+        D[k]["p%d" % h] = done(v.tensor_tensor(cols(k, "pr", h), bank(k, h), cols(k, "mk", h), OP.mult))
+
+    def sum_scalar(k, out):
+        need("s", D[k]["p0"], D[k]["p1"])
+        D[k]["t"] = done(s.activation(small(k, "dm")[:, :], small(k, "pr")[:, :], AF.Identity, accum_out=out))
+
+    def sum_vector(k, out):
+        need("v", D[k]["p0"], D[k]["p1"])
+        D[k]["t"] = done(v.tensor_reduce(out, small(k, "pr")[:, :], AxisListType.X, OP.add))
+
+    def keys(k, names):
+        return [D[k][n] for n in names]
+
+    if role == "P":
+        mask(1)
+        mask(2)
+        for k in (1, 2):
+            product(k, 0)
+            product(k, 1)
+        A2, B2 = ot["A"], ot["B"]
+        m = engines(A2, 0, NX)
+        for k in (1, 2):
+            top(k, 0)
+            top(k, 1)
+            shift(k)
+            expo(k, 0)
+            expo(k, 1)
+        putc(1)
+        puts(1)
+        putc(2)
+        pick(1, 0)
+        pick(1, 1)
+        puts(2)
+        sum_scalar(1, T.tt1[:, 0:1])
+        pick(2, 0)
+        pick(2, 1)
+        sum_vector(2, T.tt2[:, 0:1])
+        need("g", *keys(1, "cs"))
+        send(A2, T.rb[:, 0:2], T.st1[:, 0:2], "rb", m)
+        need("g", *keys(2, "cs"))
+        send(B2, T.rb[:, 0:2], T.st2[:, 0:2], "rb", m)
+        need("g", *keys(1, "t"))
+        send(A2, T.rt[:, 0:1], T.tt1[:, 0:1], "rt", m)
+        need("g", *keys(2, "t"))
+        send(B2, T.rt[:, 0:1], T.tt2[:, 0:1], "rt", m)
+    else:
+        product(2, 0)
+        mask(2)
+        top(2, 0)
+        pick(2, 0)
+        mask(1)
+        product(1, 0)
+        product(1, 1)
+        product(2, 1)
+        top(1, 0)
+        top(1, 1)
+        shift(1)
+        expo(1, 0)
+        pick(1, 1)
+        need("s", D[1]["p1"])
+        expo(1, 1)
+        putc(1)
+        need("v", D[1]["e0"])
+        pick(1, 0)
+        puts(1)
+        if role == "A":
+            R = me["RA"]
+            sum_scalar(1, T.tt1[:, 0:1])
+            need("g", *keys(1, "cs"))
+            send(R, T.ra[:, 0:2], T.st1[:, 0:2], "ra", engines(R, 0, NS))
+            need("g", *keys(1, "t"))
+            send(R, T.rt[:, 0:1], T.tt1[:, 0:1], "rt", engines(R, 0, NS))
         else:
-            need("s", kpa)
-            kta = done(s.activation(dm[:, 0:H], pr[:, 0:H], AF.Identity, accum_out=ta[:, 0:1]))
-            need("v", keb)
-            ks_ = done(v.tensor_tensor(st[:, 1:2], sa[:, 0:1], sa[:, 1:2], OP.add))
-            ktb = done(v.tensor_reduce(ta[:, 1:2], pr[:, H:NW], AxisListType.X, OP.add))
-            need("v", kta, ktb)
-            kt_ = done(v.tensor_tensor(st[:, 2:3], ta[:, 0:1], ta[:, 1:2], OP.add))
-        kst[k] = [kc_, ks_, kt_]
-        if k == 1:
-            dst = {"P": ot["A"], "A": me["RA"], "B": me["P"]}[role]
-            need("g", *kst[1])
-            send(dst, T["rb" if role == "P" else "ra"][:, 0:3], T.st1[:, 0:3], "rb" if role == "P" else "ra", engines(dst, 0, NS))
-        elif role == "P":
-            need("g", *kst[2])
-            send(ot["B"], T.rb[:, 0:3], T.st2[:, 0:3], "rb", engines(ot["B"], 0, NS))
+            sum_scalar(1, T.st1[:, 2:3])
+            need("g", *keys(1, "cst"))
+            send(me["P"], T.ra[:, 0:3], T.st1[:, 0:3], "ra", engines(me["P"], 0, NS))
+        top(2, 1)
+        shift(2)
+        need("s", D[2]["p0"])
+        expo(2, 1)
+        expo(2, 0)
+        putc(2)
+        need("v", D[2]["e1"])
+        pick(2, 1)
+        puts(2)
+        sum_vector(2, T.st2[:, 2:3])
 
     need("s", k2)
     kl = done(s.activation(T.hh[:, 1:2], T.kl[:, 0:1], AF.Ln))
+    F = T.rb
     if role == "P":
         E, ke = T.ra, [("ra", NS)]
     else:
-        E, ke = T.st2, kst[2]
+        E, ke = T.st2, keys(2, "cst")
     need("v", koa, kob, *ke)
-    kta_ = done(v.tensor_scalar(T.tha[:, 0:LEVELS], T.oa[:, 0:LEVELS], E[:, 0:1], None, OP.add))
-    ktb_ = done(v.tensor_scalar(T.thb[:, 0:LEVELS], T.ob[:, 0:LEVELS], E[:, 0:1], None, OP.add))
-    need("v", kl)
-    kh = done(v.tensor_tensor(T.hh[:, 0:1], T.hh[:, 1:2], E[:, 2:3], OP.subtract))
-    need("v", kta_, ktb_, kh, kwt, k4, ("rb", NS))
-    F = T.rb
-    kp = done(v.tensor_scalar(T.pp[:, 0:2 * LEVELS:2], T.tha[:, 0:LEVELS], F[:, 0:1], F[:, 1:2], OP.is_le, OP.mult))
-    kr = done(v.tensor_scalar(T.pp[:, 1:2 * LEVELS:2], T.thb[:, 0:LEVELS], F[:, 0:1], E[:, 1:2], OP.is_ge, OP.mult))
+    kta = done(v.tensor_scalar(T.tha[:, 0:LV], T.oa[:, 0:LV], E[:, 0:1], None, OP.add))
+    ktb = done(v.tensor_scalar(T.thb[:, 0:LV], T.ob[:, 0:LV], E[:, 0:1], None, OP.add))
+    need("v", kta, ktb, kwt, k4, ("rb", NX))
+    kp = done(v.tensor_scalar(T.pp[:, 0:2 * LV:2], T.tha[:, 0:LV], F[:, 0:1], F[:, 1:2], OP.is_le, OP.mult))
+    kr = done(v.tensor_scalar(T.pp[:, 1:2 * LV:2], T.thb[:, 0:LV], F[:, 0:1], E[:, 1:2], OP.is_ge, OP.mult))
     need("v", kp, kr)
     ksc = done(v.tensor_tensor_scan(T.sc[:, :], T.wt[:, :], T.pp[:, :], 0.0, OP.mult, OP.add))
     need("s", ksc)
-    kln = done(s.activation(T.ln[:, 0:1], T.sc[:, 2 * LEVELS - 1:2 * LEVELS], AF.Ln, scale=1.0 / 32.0))
+    kln = done(s.activation(T.ln[:, 0:1], T.sc[:, 2 * LV - 1:2 * LV], AF.Ln, scale=1.0 / 32.0))
     kz = done(v.tensor_scalar(T.bz[:, 0:1], F[:, 0:1], E[:, 0:1], SCALE, OP.max, OP.mult))
-    need("v", kz)
-    kb0 = done(v.tensor_scalar(T.bs[:, 0:1], T.bz[:, 0:1], T.hh[:, 0:1], F[:, 2:3], OP.add, OP.subtract))
-    kb1 = done(v.tensor_scalar(T.bs[:, 1:2], T.bz[:, 0:1], T.hh[:, 1:2], None, OP.add))
-    need("v", kb0, kb1, kln)
-    ky = done(v.tensor_scalar(T.yt[:, 0:2], T.bs[:, 0:2], T.ln[:, 0:1], None, OP.add))
-    need("y", ky)
+    need("v", kl)
+    kh = done(v.tensor_tensor(T.hh[:, 0:1], T.hh[:, 1:2], E[:, 2:3], OP.subtract))
+    need("v", kz, kh)
+    kb = done(v.tensor_scalar(T.bs[:, 0:2], T.hh[:, 0:2], T.bz[:, 0:1], None, OP.add))
+    need("v", kb, kln)
+    ky1 = done(v.tensor_scalar(T.yt[:, 1:2], T.bs[:, 1:2], T.ln[:, 0:1], None, OP.add))
+    need("v", ("rt", NX))
+    ky0 = done(v.tensor_scalar(T.yt[:, 0:1], T.bs[:, 0:1], T.ln[:, 0:1], T.rt[:, 0:1], OP.add, OP.subtract))
+    need("y", ky0, ky1)
     kyo = done(y.dma_start(T.y[:, :], T.yt[:, 0:2]), 16)
     need("y", kyo)
 

@@ -4,46 +4,51 @@ from concourse.mybir import dt, AluOpType as OP, AxisListType, ActivationFunctio
 
 SIM_CORES = 16
 NC = 192
-NW = 3 * NC
-H = NW // 2
+BANK = 512
 SCALE = float(np.float32(0.03))
-GRID = 256.0
-MAGIC = 1.5 * 2.0 ** 23 * GRID
-STEP = SCALE * GRID
-KSTEP = float(np.exp(-STEP))
-LV = 4
 
-NX1 = 8
+KP = 10
+DEG = 6
+ND = DEG + 1
+LN2 = float(np.log(2.0))
+_xx = 1.5025 + 0.5075 * np.cos(np.pi * (np.arange(200) + 0.5) / 200)
+POLY = [float(c) for c in np.polyfit(_xx, np.log(_xx), DEG)]
+
 NX = 8
-ND = 8
-NWE = 16
-NS = 16
+NI = 16
+NPW = 8
 
-NK = 110
+NK = 100
 SCRATCH = {
     "xb": ("sbuf", [128, 512], "bfloat16"),
     "wb": ("sbuf", [128, 768], "bfloat16"),
     "xq": ("sbuf", [128, 128], "float8_e4m3fn_x4"),
     "xs": ("sbuf", [128, 128], "uint8"),
-    "wq": ("sbuf", [128, NW], "float8_e4m3fn_x4"),
-    "ws": ("sbuf", [128, NW], "uint8"),
-    "cid": ("sbuf", [128, NW], "float32"),
-    "ps": ("psum", [128, 2048], "float32"),
+    "fq": ("sbuf", [128, 128], "float8_e4m3fn_x4"),
+    "fs": ("sbuf", [128, 128], "uint8"),
+    "wq": ("sbuf", [128, 3 * NC], "float8_e4m3fn_x4"),
+    "ws": ("sbuf", [128, 3 * NC], "uint8"),
+    "lq": ("sbuf", [128, 2 * NC], "float8_e4m3fn_x4"),
+    "lz": ("sbuf", [128, 2 * NC], "uint8"),
+    "cid": ("sbuf", [128, NC], "float32"),
+    "mk": ("sbuf", [128, 6 * NC], "float32"),
+    "pr": ("sbuf", [128, 6 * NC + 8], "float32"),
+    "ex": ("sbuf", [128, 6 * NC], "float32"),
+    "dm": ("sbuf", [128, 6 * NC + 8], "float32"),
+    "ps": ("psum", [128, 6 * BANK], "float32"),
+    "tgd": ("dram", [128, 2], "bfloat16"),
 }
-for _k in ("1", "2"):
-    SCRATCH["f%sq" % _k] = ("sbuf", [128, 128], "float8_e4m3fn_x4")
-    SCRATCH["f%ss" % _k] = ("sbuf", [128, 128], "uint8")
-    for _n in ("mk", "pr", "ex", "dm"):
-        SCRATCH[_n + _k] = ("sbuf", [128, NW], "float32")
-    for _n in ("ix", "mx", "qq", "nb", "sa", "st", "tt"):
-        SCRATCH[_n + _k] = ("sbuf", [128, 8], "float32")
-for _n in ("tgb", "tg1", "tg2"):
+for _n in ("tgo", "tgf"):
     SCRATCH[_n] = ("sbuf", [128, 16], "bfloat16")
-for _n in ("tgd", "td1"):
-    SCRATCH[_n] = ("dram", [128, 2], "bfloat16")
-for _n in ("ra", "rb", "rt", "oa", "ob", "kc", "kl", "wt", "tha", "thb", "hh", "pp", "sc", "bz", "bs", "ln", "yt"):
+for _n in ("ix1", "ix2", "mx", "nb1", "nb2", "nb3", "sa", "st1", "rb", "rt", "yt", "tt", "mm", "ww", "pa", "ub", "us", "xv", "hs",
+           "gg", "nn", "zb", "on", "cf"):
     SCRATCH[_n] = ("sbuf", [128, 8], "float32")
-SEMAPHORES = ["tg1", "tg2", "f1c", "f1s", "f2c", "f2s", "aw", "ra", "rb", "rt", "ls"] + ["k%d" % i for i in range(NK)]
+for _n in ("lt", "zz", "lk", "thr", "hv", "ck", "vb", "fe"):
+    SCRATCH[_n] = ("sbuf", [128, 16], "float32")
+_REM = ["tgf", "xc", "xs", "wcP", "wsP"] + [a + b for a in ("wc", "ws", "lc", "lz") for b in "AB"] + ["rb", "rt", "ls"]
+SEMAPHORES = _REM + ["k%d" % i for i in range(NK)]
+SLOT = {"A": 0, "P": 1, "B": 2}
+LATE = {"A": (0, NC), "B": (NC, 2 * NC)}
 
 
 def plan(T, topo):
@@ -55,9 +60,9 @@ def plan(T, topo):
         P = [c for c in here if all(topo.may_write(c, d) for d in there)][0]
         A, B = sorted([c for c in here if c != P], key=lambda c: topo.die(c) != topo.die(P))
         helpers = [c for c in range(SIM_CORES) if topo.chip(c) == ch and T.rank_of(c) is None and all(topo.may_write(c, d) for d in there)]
-        RA = sorted(helpers, key=lambda c: topo.die(c) != topo.die(A))[0]
-        RB = sorted([c for c in helpers if c != RA], key=lambda c: topo.die(c) != topo.die(B))[0]
-        out[ch] = {"P": P, "A": A, "B": B, "RA": RA, "RB": RB, "base": min(T.rank_of(c) for c in here), "here": here}
+        hB = sorted(helpers, key=lambda c: topo.die(c) != topo.die(B))[:2]
+        hA = [c for c in helpers if c not in hB][0]
+        out[ch] = {"P": P, "A": A, "B": B, "relA": [P, hA], "relB": hB}
     return chips, out
 
 
@@ -66,10 +71,7 @@ def rank_program(g, core, T, topo):
     ch = topo.chip(core)
     me = plans[ch]
     ot = plans[[c for c in chips if c != ch][0]]
-    role = [r for r in ("P", "A", "B", "RA", "RB") if me[r] == core]
-    if not role:
-        return
-    role = role[0]
+    mates = [ot["A"], ot["B"]]
     Q = {"g": g, "v": g.vector, "t": g.tensor, "s": g.scalar, "y": g.sync}
     seen, made, sent = set(), [], [0]
 
@@ -109,253 +111,331 @@ def rank_program(g, core, T, topo):
     def u8(v):
         return v.bitcast(dt.uint8)
 
-    if role in ("RA", "RB"):
-        dst = ot["P"]
-        k = "1" if role == "RA" else "2"
-        m = engines(dst, 0, NX)
-        need("g", ("tg1", 1))
-        send(dst, T["tg" + k][:, 0:2], T.td1[:, :], "tg" + k, m)
-        need("g", ("f1c", NX1))
-        send(dst, u8(T["f%sq" % k][:, :]), u8(T.f1q[:, :]), "f%sc" % k, m)
-        need("g", ("f1s", NX1))
-        send(dst, T["f%ss" % k][:, :], T.f1s[:, :], "f%ss" % k, m)
-        if role == "RA":
-            need("g", ("ra", NS))
-            send(dst, T.rb[:, 0:2], T.ra[:, 0:2], "rb", m)
-            need("g", ("rt", NS))
-            send(dst, T.rt[:, 0:1], T.rt[:, 0:1], "rt", m)
-        need("g", ("ls", sent[0]))
-        return
+    def W(r):
+        lo = SLOT[r] * NC
+        return T.wq[:, lo:lo + NC], T.ws[:, lo:lo + NC]
 
+    def relay(r):
+        lo, hi = LATE[r]
+        q, z = W(r)
+        rel = me["rel" + r]
+        dst = mates[rel.index(core)]
+        m = engines(dst, 0, NX)
+        if core != me["P"]:
+            need("g", ("ws" + r, NI))
+            send(dst, T.lz[:, lo:hi], z, "lz" + r, m)
+        need("g", ("wc" + r, NI))
+        send(dst, u8(T.lq[:, lo:hi]), u8(q), "lc" + r, m)
+        if core != me["P"] and me["P"] in rel:
+            send(mates[rel.index(me["P"])], T.lz[:, lo:hi], z, "lz" + r, m)
+
+    role = [r for r in "PAB" if me[r] == core]
+    if not role:
+        for r in "AB":
+            if core in me["rel" + r]:
+                relay(r)
+                need("g", ("ls", sent[0]))
+        return
+    role = role[0]
     v, s, t, y = g.vector, g.scalar, g.tensor, g.sync
-    base = me["base"]
-    slot = (T.rank_of(core) - base) * NC
-    wq = T.wq[:, slot:slot + NC]
-    ws = T.ws[:, slot:slot + NC]
+    wq, ws = W(role)
 
     ktd = done(s.dma_start(T.tgd[:, :], T.tg[:, :]), 16)
-    kx = done(y.dma_start(T.xb[:, :], T.x[:, :]), 16)
-    kw = done(y.dma_start(T.wb[:, :], T.w[:, :]), 16)
+    K = {}
+    for n in ("xw" if role == "P" else "wx"):
+        K[n] = done(y.dma_start(T[n + "b"][:, :], T[n][:, :]), 16)
+    ktg = done(s.dma_start(T.tgo[:, 0:2], T.tg[:, :]), 16)
+    kio = done(g.iota(T.cid[:, :], [[1, NC]], 0, 0, allow_small_or_imprecise_dtypes=True))
+
+    k0 = done(v.memset(T.lt[:, 0:KP], LN2))
+    kzz = done(v.memset(T.zz[:, 0:KP], 0.0))
+    need("v", k0, kzz)
+    klk = done(v.tensor_tensor_scan(T.lk[:, 0:KP], T.lt[:, 0:KP], T.zz[:, 0:KP], 0.0, OP.add, OP.add))
+    need("s", klk)
+    kthr = done(s.activation(T.thr[:, 0:KP], T.lk[:, 0:KP], AF.Exp))
+
+    def quant(n, q, z):
+        need("v", K[n])
+        return done(v.quantize_mx(q, z, T[n + "b"][:, :]))
+
+    if role == "P":
+        kqx = quant("x", T.xq[:, :], T.xs[:, :])
+    kqw = quant("w", wq, ws)
     if role != "P":
-        ktg = done(s.dma_start(T.tgb[:, 0:2], T.tg[:, :]), 16)
+        kqx = quant("x", T.xq[:, :], T.xs[:, :])
 
-    kio = [done(g.iota(T.cid[:, 0:NC], [[1, NC]], base * NC, 0, allow_small_or_imprecise_dtypes=True))]
-    k0 = done(v.memset(T.kc[:, 0:1], -STEP - float(np.log(1.0 - KSTEP))))
-    k1 = done(v.memset(T.kc[:, 1:LV - 1], -STEP))
-    k2 = done(v.memset(T.kl[:, 0:1], 32.0 * (1.0 - KSTEP)))
-    k3 = done(v.memset(T.wt[:, :], 1.0))
-    need("v", k3)
-    k4 = done(v.memset(T.wt[:, 0:1], 0.0))
-    need("s", k0, k1, k3)
-    kwt = done(s.activation(T.wt[:, 2:2 * LV:2], T.kc[:, 0:LV - 1], AF.Exp))
-    need("v", kio[0])
-    for j in (1, 2):
-        kio.append(done(v.tensor_scalar(T.cid[:, NC * j:NC * (j + 1)], T.cid[:, 0:NC], float(NC * j), None, OP.add)))
-
-    need("v", kx)
-    kqx = done(v.quantize_mx(T.xq[:, :], T.xs[:, :], T.xb[:, :]))
-    need("v", kw)
-    kqw = done(v.quantize_mx(wq, ws, T.wb[:, :]))
-
-    others = [c for c in me["here"] if c != core]
     need("g", ktd)
     if role == "P":
-        A2, B1 = ot["A"], me["B"]
-        m1, m2 = engines(A2, 0, NX), engines(B1, NX, ND)
-        fused(([A2], T.td1[:, :], T.tgd[:, :], "tg1", engines(A2, 0, 1)), ([B1], T.td1[:, :], T.tgd[:, :], "tg1", engines(B1, NX, 1)))
+        other, B2, A1 = ot["P"], ot["B"], me["A"]
+        m = engines(other, 0, NX)
+        mi = engines(A1, NX, NPW)
+        send(other, T.tgf[:, 0:2], T.tgd[:, :], "tgf", m)
         need("g", kqx)
-        fused(([A2], u8(T.f1q[:, :]), u8(T.xq[:, :]), "f1c", m1), ([B1], u8(T.f1q[:, :]), u8(T.xq[:, :]), "f1c", m2))
-        fused(([A2], T.f1s[:, :], T.xs[:, :], "f1s", m1), ([B1], T.f1s[:, :], T.xs[:, :], "f1s", m2))
+        send(other, u8(T.fq[:, :]), u8(T.xq[:, :]), "xc", m)
+        send(other, T.fs[:, :], T.xs[:, :], "xs", m)
+        need("g", kqw)
+        fused(([B2], u8(wq), u8(wq), "wcP", m), ([A1], u8(wq), u8(wq), "wcP", mi))
+        fused(([B2], ws, ws, "wsP", m), ([A1], ws, ws, "wsP", mi))
+        for r in "AB":
+            if core in me["rel" + r]:
+                relay(r)
+        nf, nwp = NX, None
     else:
-        R = me["R" + role]
-        m1 = engines(R, 0, NX1)
-        send(R, T.td1[:, :], T.tgd[:, :], "tg1", engines(R, 0, 1))
+        other = me["B" if role == "A" else "A"]
+        rel = me["rel" + role]
+        m = engines(other, 0, NI)
+        send(other, T.tgf[:, 0:2], T.tgd[:, :], "tgf", m)
+        need("g", kqw)
+        fused((rel, ws, ws, "ws" + role, m))
+        fused((rel, u8(wq), u8(wq), "wc" + role, m))
         need("g", kqx)
-        send(R, u8(T.f1q[:, :]), u8(T.xq[:, :]), "f1c", m1)
-        send(R, T.f1s[:, :], T.xs[:, :], "f1s", m1)
-    mw = engines(others[0], 0, NWE)
-    need("g", kqw)
-    fused((others, u8(wq), u8(wq), "aw", mw))
-    fused((others, ws, ws, "aw", mw))
-    kaw = ("aw", 2 * 2 * NWE)
-    G = int(GRID)
-    koa = done(g.iota(T.oa[:, 0:LV], [[G, LV]], -G * (LV - 1), 0, allow_small_or_imprecise_dtypes=True))
-    kob = done(g.iota(T.ob[:, 0:LV], [[-G, LV]], G * (LV - 1), 0, allow_small_or_imprecise_dtypes=True))
+        send(other, u8(T.fq[:, :]), u8(T.xq[:, :]), "xc", m)
+        send(other, T.fs[:, :], T.xs[:, :], "xs", m)
+        if me["P"] not in rel:
+            send(me["P"], u8(wq), u8(wq), "wc" + role, m)
+            send(me["P"], ws, ws, "ws" + role, m)
+        nf, nwp = NI, (NPW if role == "A" else NX)
 
-    halves = [(0, H), (H, NW)]
-    if role == "P":
-        sets = {k: (T["f%dq" % k], T["f%ds" % k], [kaw, ("f%dc" % k, NX), ("f%ds" % k, NX)], T["tg%d" % k], ("tg%d" % k, NX), halves) for k in (1, 2)}
-    else:
-        n1 = ND if role == "B" else NX
-        need("y", ("tg1", 1))
-        kt1 = done(y.dma_start(T.tg1[:, 0:2], T.td1[:, :]), 16)
-        sets = {1: (T.f1q, T.f1s, [kaw, ("f1c", n1), ("f1s", n1)], T.tg1, kt1, halves),
-                2: (T.xq, T.xs, [kqx], T.tgb, ktg, [(slot, slot + NC), (NC, NW) if slot == 0 else (0, NW - NC)])}
-    D = {1: {}, 2: {}}
+    own, far = (T.xq[:, :], T.xs[:, :], [kqx]), (T.fq[:, :], T.fs[:, :], [("xc", nf), ("xs", nf)])
+    B = []
 
-    def bank(k, h):
-        b = 1024 * (k - 1) + 512 * h
-        lo, hi = sets[k][5][h]
-        return T.ps[:, b:b + hi - lo]
-
-    def cols(k, name, h):
-        lo, hi = sets[k][5][h]
-        return T[name + "%d" % k][:, lo:hi]
-
-    def small(k, name):
-        return T[name + "%d" % k]
-
-    def mask(k):
-        tg, ix = sets[k][3], small(k, "ix")
-        need("v", sets[k][4])
-        ki = done(v.tensor_scalar(ix[:, 0:1], tg[:, 0:1], float(NC), tg[:, 1:2], OP.mult, OP.add))
-        need("v", ki, *kio)
-        D[k]["m"] = done(v.tensor_scalar(small(k, "mk")[:, :], T.cid[:, :], ix[:, 0:1], SCALE, OP.is_equal, OP.mult))
-
-    def product(k, h):
-        need("t", kqw, *sets[k][2])
-        lo, hi = sets[k][5][h]
-        D[k]["mm%d" % h] = done(t.matmul_mx(bank(k, h), sets[k][0][:, :], sets[k][1][:, :], T.wq[:, lo:hi], T.ws[:, lo:hi], True, True))
-
-    def top(k, h):
-        need("v", D[k]["mm%d" % h])
-        D[k]["x%d" % h] = done(v.tensor_reduce(small(k, "mx")[:, h:h + 1], bank(k, h), AxisListType.X, OP.max))
-
-    def shift(k):
-        mx, qq = small(k, "mx"), small(k, "qq")
-        need("v", D[k]["x0"], D[k]["x1"])
-        kq = done(v.tensor_scalar(qq[:, 0:1], mx[:, 0:1], mx[:, 1:2], MAGIC, OP.max, OP.add))
-        need("v", kq)
-        D[k]["nb"] = done(v.tensor_scalar(small(k, "nb")[:, 0:1], qq[:, 0:1], MAGIC, -SCALE, OP.subtract, OP.mult))
-
-    def putc(k):
-        D[k]["c"] = done(v.tensor_scalar(small(k, "st")[:, 0:1], small(k, "qq")[:, 0:1], MAGIC, None, OP.subtract))
-
-    def expo(k, h):
-        need("s", D[k]["nb"])
-        D[k]["e%d" % h] = done(s.activation(cols(k, "ex", h), bank(k, h), AF.Exp, bias=small(k, "nb")[:, 0:1], scale=SCALE,
-                                            accum_out=small(k, "sa")[:, h:h + 1]))
-
-    def puts(k):
-        need("v", D[k]["e0"], D[k]["e1"])
-        D[k]["s"] = done(v.tensor_tensor(small(k, "st")[:, 1:2], small(k, "sa")[:, 0:1], small(k, "sa")[:, 1:2], OP.add))
-
-    def pick(k, h):
-        need("v", D[k]["m"])
-        D[k]["p%d" % h] = done(v.tensor_tensor(cols(k, "pr", h), bank(k, h), cols(k, "mk", h), OP.mult))
-
-    def sum_scalar(k, out):
-        need("s", D[k]["p0"], D[k]["p1"])
-        D[k]["t"] = done(s.activation(small(k, "dm")[:, :], small(k, "pr")[:, :], AF.Identity, accum_out=out))
-
-    def sum_vector(k, out):
-        need("v", D[k]["p0"], D[k]["p1"])
-        D[k]["t"] = done(v.tensor_reduce(out, small(k, "pr")[:, :], AxisListType.X, OP.add))
-
-    def keys(k, names):
-        return [D[k][n] for n in names]
-
-    if role == "P":
-        mask(1)
-        mask(2)
-        for k in (1, 2):
-            product(k, 0)
-            product(k, 1)
-        A2, B2 = ot["A"], ot["B"]
-        m = engines(A2, 0, NX)
-        for k in (1, 2):
-            top(k, 0)
-            top(k, 1)
-            shift(k)
-            expo(k, 0)
-            expo(k, 1)
-        putc(1)
-        puts(1)
-        putc(2)
-        pick(1, 0)
-        pick(1, 1)
-        puts(2)
-        sum_scalar(1, T.tt1[:, 0:1])
-        pick(2, 0)
-        pick(2, 1)
-        sum_vector(2, T.tt2[:, 0:1])
-        need("g", *keys(1, "cs"))
-        send(A2, T.rb[:, 0:2], T.st1[:, 0:2], "rb", m)
-        need("g", *keys(2, "cs"))
-        send(B2, T.rb[:, 0:2], T.st2[:, 0:2], "rb", m)
-        need("g", *keys(1, "t"))
-        send(A2, T.rt[:, 0:1], T.tt1[:, 0:1], "rt", m)
-        need("g", *keys(2, "t"))
-        send(B2, T.rt[:, 0:1], T.tt2[:, 0:1], "rt", m)
-    else:
-        product(2, 0)
-        mask(2)
-        top(2, 0)
-        pick(2, 0)
-        mask(1)
-        product(1, 0)
-        product(1, 1)
-        product(2, 1)
-        top(1, 0)
-        top(1, 1)
-        shift(1)
-        expo(1, 0)
-        pick(1, 1)
-        need("s", D[1]["p1"])
-        expo(1, 1)
-        putc(1)
-        need("v", D[1]["e0"])
-        pick(1, 0)
-        puts(1)
-        if role == "A":
-            R = me["RA"]
-            sum_scalar(1, T.tt1[:, 0:1])
-            need("g", *keys(1, "cs"))
-            send(R, T.ra[:, 0:2], T.st1[:, 0:2], "ra", engines(R, 0, NS))
-            need("g", *keys(1, "t"))
-            send(R, T.rt[:, 0:1], T.tt1[:, 0:1], "rt", engines(R, 0, NS))
+    def block(X, r, late=False):
+        if late:
+            lo, hi = LATE[r]
+            B.append((X, T.lq[:, lo:hi], T.lz[:, lo:hi], [("lz" + r, NX), ("lc" + r, NX)], T.rank_of(ot[r])))
         else:
-            sum_scalar(1, T.st1[:, 2:3])
-            need("g", *keys(1, "cst"))
-            send(me["P"], T.ra[:, 0:3], T.st1[:, 0:3], "ra", engines(me["P"], 0, NS))
-        top(2, 1)
-        shift(2)
-        need("s", D[2]["p0"])
-        expo(2, 1)
-        expo(2, 0)
-        putc(2)
-        need("v", D[2]["e1"])
-        pick(2, 1)
-        puts(2)
-        sum_vector(2, T.st2[:, 2:3])
+            q, z = W(r)
+            if r == role:
+                ks = [kqw]
+            else:
+                n = nwp if r == "P" else NI
+                ks = [("wc" + r, n), ("ws" + r, n)]
+            B.append((X, q, z, ks, T.rank_of((ot if r == "P" and role == "B" else me)[r])))
 
-    need("s", k2)
-    kl = done(s.activation(T.hh[:, 1:2], T.kl[:, 0:1], AF.Ln))
-    F = T.rb
     if role == "P":
-        E, ke = T.ra, [("ra", NS)]
+        SET = {1: (0, 3), 2: (3, 6)}
+        for X in (far, own):
+            for r in "PAB":
+                block(X, r)
+        gaps = (2, 5)
     else:
-        E, ke = T.st2, keys(2, "cst")
-    need("v", koa, kob, *ke)
-    kta = done(v.tensor_scalar(T.tha[:, 0:LV], T.oa[:, 0:LV], E[:, 0:1], None, OP.add))
-    ktb = done(v.tensor_scalar(T.thb[:, 0:LV], T.ob[:, 0:LV], E[:, 0:1], None, OP.add))
-    need("v", kta, ktb, kwt, k4, ("rb", NX))
-    kp = done(v.tensor_scalar(T.pp[:, 0:2 * LV:2], T.tha[:, 0:LV], F[:, 0:1], F[:, 1:2], OP.is_le, OP.mult))
-    kr = done(v.tensor_scalar(T.pp[:, 1:2 * LV:2], T.thb[:, 0:LV], F[:, 0:1], E[:, 1:2], OP.is_ge, OP.mult))
-    need("v", kp, kr)
-    ksc = done(v.tensor_tensor_scan(T.sc[:, :], T.wt[:, :], T.pp[:, :], 0.0, OP.mult, OP.add))
-    need("s", ksc)
-    kln = done(s.activation(T.ln[:, 0:1], T.sc[:, 2 * LV - 1:2 * LV], AF.Ln, scale=1.0 / 32.0))
-    kz = done(v.tensor_scalar(T.bz[:, 0:1], F[:, 0:1], E[:, 0:1], SCALE, OP.max, OP.mult))
-    need("v", kl)
-    kh = done(v.tensor_tensor(T.hh[:, 0:1], T.hh[:, 1:2], E[:, 2:3], OP.subtract))
-    need("v", kz, kh)
-    kb = done(v.tensor_scalar(T.bs[:, 0:2], T.hh[:, 0:2], T.bz[:, 0:1], None, OP.add))
-    need("v", kb, kln)
-    ky1 = done(v.tensor_scalar(T.yt[:, 1:2], T.bs[:, 1:2], T.ln[:, 0:1], None, OP.add))
-    need("v", ("rt", NX))
-    ky0 = done(v.tensor_scalar(T.yt[:, 0:1], T.bs[:, 0:1], T.ln[:, 0:1], T.rt[:, 0:1], OP.add, OP.subtract))
-    need("y", ky0, ky1)
+        SET = {1: (0, 2), 2: (2, 4), 3: (4, 6)}
+        for X in (far, own):
+            block(X, role)
+            block(X, "P")
+        block(own, "A", True)
+        block(own, "B", True)
+        gaps = (1, 3, 4)
+    at = [NC * i + sum(1 for j in gaps if j <= i) for i in range(6)]
+    after = set()
+    D = {}
+
+    def bank(i):
+        return T.ps[:, BANK * i:BANK * i + NC]
+
+    def index(k):
+        ix, tg = T["ix%d" % k], (T.tgf if k == 1 else T.tgo)
+        need("v", ("tgf", nf) if k == 1 else ktg)
+        D["ix%d" % k] = done(v.tensor_scalar(ix[:, 0:1], tg[:, 0:1], float(NC), tg[:, 1:2], OP.mult, OP.add))
+
+    def mask(k, i):
+        need("v", kio, D["ix%d" % k])
+        D["m%d" % i] = done(v.tensor_scalar(T.mk[:, NC * i:NC * (i + 1)], T.cid[:, :], T["ix%d" % k][:, 0:1], -float(NC * B[i][4]), OP.subtract, OP.is_equal))
+
+    def product(i):
+        X, q, z, ks, _ = B[i]
+        need("t", *X[2])
+        need("t", *ks)
+        D["p%d" % i] = done(t.matmul_mx(bank(i), X[0], X[1], q, z, True, True))
+
+    def top(i):
+        need("v", D["p%d" % i])
+        D["x%d" % i] = done(v.tensor_reduce(T.mx[:, i:i + 1], bank(i), AxisListType.X, OP.max))
+
+    def pick(i):
+        need("v", D["m%d" % i], D["p%d" % i])
+        if i in after:
+            need("v", D["e%d" % i])
+        D["k%d" % i] = done(v.tensor_tensor(T.pr[:, at[i]:at[i] + NC], bank(i), T.mk[:, NC * i:NC * (i + 1)], OP.mult))
+
+    def expo(i, k):
+        need("s", D["nb%d" % k], D["k%d" % i] if i not in after else D["x%d" % i])
+        D["e%d" % i] = done(s.activation(T.ex[:, NC * i:NC * (i + 1)], bank(i), AF.Exp, bias=T["nb%d" % k][:, 0:1], scale=SCALE, accum_out=T.sa[:, i:i + 1]))
+
+    def gather(lo, hi, name, *keys, out=None):
+        a, b = at[lo] - (1 if keys else 0), at[hi - 1] + NC
+        need("s", *keys)
+        need("s", *[D["k%d" % i] for i in range(lo, hi)])
+        if out is None:
+            D[name] = done(s.activation(T.dm[:, a:b], T.pr[:, a:b], AF.Identity, accum_out=T.pr[:, at[hi] - 1:at[hi]]))
+        else:
+            D[name] = done(s.activation(T.dm[:, a:b], T.pr[:, a:b], AF.Identity, scale=SCALE, accum_out=out))
+
+    def shift(k, st, o):
+        lo, hi = SET[k]
+        nb = T["nb%d" % k]
+        need("v", *[D["x%d" % i] for i in range(lo, hi)])
+        if hi - lo == 2:
+            D["nb%d" % k] = done(v.tensor_scalar(nb[:, 0:1], T.mx[:, lo:lo + 1], T.mx[:, lo + 1:lo + 2], -SCALE, OP.max, OP.mult))
+            D["c%d" % k] = done(v.tensor_tensor(st[:, o:o + 1], T.mx[:, lo:lo + 1], T.mx[:, lo + 1:lo + 2], OP.max))
+        else:
+            D["c%d" % k] = done(v.tensor_scalar(st[:, o:o + 1], T.mx[:, lo:lo + 1], T.mx[:, lo + 1:lo + 2], T.mx[:, lo + 2:lo + 3], OP.max, OP.max))
+            need("v", D["c%d" % k])
+            D["nb%d" % k] = done(v.tensor_scalar(nb[:, 0:1], st[:, o:o + 1], -SCALE, None, OP.mult))
+
+    def total(k, st, o):
+        lo, hi = SET[k]
+        need("v", *[D["e%d" % i] for i in range(lo, hi)])
+        if hi - lo == 2:
+            D["s%d" % k] = done(v.tensor_tensor(st[:, o + 1:o + 2], T.sa[:, lo:lo + 1], T.sa[:, lo + 1:lo + 2], OP.add))
+        else:
+            D["s%d" % k] = done(v.tensor_scalar(st[:, o + 1:o + 2], T.sa[:, lo:lo + 1], T.sa[:, lo + 1:lo + 2], T.sa[:, lo + 2:lo + 3], OP.add, OP.add))
+
+    def share():
+        need("g", D["c1"], D["s1"])
+        send(other, T.rb[:, 0:2], T.st1[:, 0:2], "rb", m)
+        need("g", D["t1"])
+        send(other, T.rt[:, 0:1], T.tt[:, 0:1], "rt", m)
+
+    def tables():
+        kh0 = done(v.memset(T.hv[:, 0:KP], 0.5))
+        ks = [done(v.memset(T.on[:, 0:ND], 1.0))]
+        need("v", kh0)
+        kc = done(v.tensor_tensor_scan(T.ck[:, 0:KP], T.hv[:, 0:KP], T.zz[:, 0:KP], 0.5, OP.mult, OP.add))
+        need("v", kc)
+        ks.append(done(v.memset(T.ck[:, KP - 1:KP], 2.0 ** -KP)))
+        for j, c in enumerate(POLY):
+            ks.append(done(v.memset(T.cf[:, j:j + 1], c)))
+        return ks
+
+    def weights():
+        need("s", ("rb", nf), D["c2"], D["nb3"])
+        D["w"] = done(s.activation(T.ww[:, 0:2], T.rb[:, 0:8:4], AF.Exp, bias=T.nb3[:, 0:1], scale=SCALE))
+
+    def early():
+        need("v", D["w"], D["s2"])
+        kpa = done(v.tensor_tensor(T.pa[:, 0:2], T.ww[:, 0:2], T.rb[:, 1:8:4], OP.mult))
+        need("v", kpa, *ktab)
+        D["ub"] = done(v.tensor_scalar(T.ub[:, 0:ND], T.on[:, 0:ND], T.pa[:, 0:1], T.pa[:, 1:2], OP.mult, OP.add))
+
+    def base():
+        need("v", D["nb3"])
+        D["zb"] = done(v.tensor_scalar(T.zb[:, 0:1], T.nb3[:, 0:1], -1.0, KP * LN2, OP.mult, OP.add))
+
+    def finish(u, ku, add, kt):
+        ks = [ku, kthr] + ([] if add is None else [add[1]])
+        need("v", *ks)
+        if add is None:
+            kvb = done(v.tensor_scalar(T.vb[:, 0:KP], T.thr[:, 0:KP], u[:, 0:1], None, OP.is_gt))
+        else:
+            kvb = done(v.tensor_scalar(T.vb[:, 0:KP], T.thr[:, 0:KP], add[0], u[:, 0:1], OP.subtract, OP.is_gt))
+        need("v", kvb)
+        kfe = done(v.tensor_tensor_scan(T.fe[:, 0:KP], T.vb[:, 0:KP], T.ck[:, 0:KP], 0.5, OP.mult, OP.add))
+        knn = done(v.tensor_reduce(T.nn[:, 0:1], T.vb[:, 0:KP], AxisListType.X, OP.add))
+        need("v", kfe)
+        if add is None:
+            kxv = done(v.tensor_scalar(T.xv[:, 0:ND], u[:, 0:ND], T.fe[:, KP - 1:KP], None, OP.mult))
+        else:
+            kxv = done(v.tensor_scalar(T.xv[:, 0:ND], u[:, 0:ND], add[0], T.fe[:, KP - 1:KP], OP.add, OP.mult))
+        need("v", knn, D["zb"])
+        kg1 = done(v.tensor_scalar(T.gg[:, 1:2], T.nn[:, 0:1], -LN2, T.zb[:, 0:1], OP.mult, OP.add))
+        need("v", kxv)
+        khs = done(v.tensor_tensor_scan(T.hs[:, 0:ND], T.xv[:, 0:ND], T.cf[:, 0:ND], 0.0, OP.mult, OP.add))
+        need("v", kg1, kt, ("rt", nf))
+        kg0 = done(v.tensor_scalar(T.gg[:, 0:1], T.gg[:, 1:2], T.tt[:, 1:2], T.rt[:, 0:1], OP.subtract, OP.subtract))
+        need("v", khs, kg0)
+        return done(v.tensor_scalar(T.yt[:, 0:2], T.gg[:, 0:2], T.hs[:, ND - 1:ND], None, OP.add))
+
+    index(2)
+    for i in range(*SET[2]):
+        mask(2, i)
+    if role == "P":
+        for i in (3, 4, 0, 1, 5, 2):
+            product(i)
+        top(3)
+        pick(3)
+        ktab = tables()
+        index(1)
+        for i in (0, 1, 2):
+            mask(1, i)
+        top(4)
+        pick(4)
+        gather(3, 5, "g2")
+        top(0)
+        pick(0)
+        top(1)
+        pick(1)
+        gather(0, 2, "g1")
+        top(2)
+        shift(1, T.st1, 0)
+        pick(2)
+        for i in (0, 1, 2):
+            expo(i, 1)
+        top(5)
+        shift(2, T.rb, 4)
+        total(1, T.st1, 0)
+        pick(5)
+        gather(2, 3, "t1", D["g1"], out=T.tt[:, 0:1])
+        share()
+        for i in (3, 4, 5):
+            expo(i, 2)
+        gather(5, 6, "t2", D["g2"], out=T.tt[:, 1:2])
+        total(2, T.rb, 4)
+        need("v", D["c2"], ("rb", nf))
+        D["nb3"] = done(v.tensor_scalar(T.nb3[:, 0:1], T.rb[:, 0:1], T.rb[:, 4:5], -SCALE, OP.max, OP.mult))
+        weights()
+        base()
+        early()
+        ky = finish(T.ub, D["ub"], None, D["t2"])
+    else:
+        for i in (2, 0, 1, 3, 4, 5):
+            product(i)
+        mask(2, 4)
+        mask(2, 5)
+        ktab = tables()
+        top(2)
+        pick(2)
+        gather(2, 3, "g2")
+        index(1)
+        mask(1, 0)
+        mask(1, 1)
+        top(0)
+        pick(0)
+        gather(0, 1, "g1")
+        top(1)
+        shift(1, T.st1, 0)
+        pick(1)
+        expo(0, 1)
+        expo(1, 1)
+        gather(1, 2, "t1", D["g1"], out=T.tt[:, 0:1])
+        top(3)
+        shift(2, T.rb, 4)
+        total(1, T.st1, 0)
+        pick(3)
+        share()
+        expo(2, 2)
+        expo(3, 2)
+        gather(3, 4, "g3", D["g2"])
+        top(4)
+        total(2, T.rb, 4)
+        need("v", D["x4"], D["c2"], ("rb", nf))
+        km = done(v.tensor_scalar(T.mm[:, 0:1], T.mx[:, 4:5], T.rb[:, 0:1], T.rb[:, 4:5], OP.max, OP.max))
+        top(5)
+        need("v", km, D["x5"])
+        D["nb3"] = done(v.tensor_scalar(T.nb3[:, 0:1], T.mx[:, 5:6], T.mm[:, 0:1], -SCALE, OP.max, OP.mult))
+        pick(5)
+        after.add(4)
+        weights()
+        expo(4, 3)
+        expo(5, 3)
+        early()
+        pick(4)
+        gather(4, 6, "t3", D["g3"], out=T.tt[:, 1:2])
+        need("v", D["ub"], D["e4"])
+        kus = done(v.tensor_scalar(T.us[:, 0:ND], T.ub[:, 0:ND], T.sa[:, 4:5], None, OP.add))
+        base()
+        ky = finish(T.us, kus, (T.sa[:, 5:6], D["e5"]), D["t3"])
+    need("y", ky)
     kyo = done(y.dma_start(T.y[:, :], T.yt[:, 0:2]), 16)
     need("y", kyo)
 

import numpy as np
from concourse.bass import DstId, RemoteDMATransfer
from concourse.mybir import dt, AluOpType as OP, AxisListType, ActivationFunctionType as AF

SIM_CORES = 16
NC = 192
BANK = 512
SCALE = float(np.float32(0.03))

KP = 10
DEG = 6
ND = DEG + 1
LN2 = float(np.log(2.0))
_xx = 1.5025 + 0.5075 * np.cos(np.pi * (np.arange(200) + 0.5) / 200)
POLY = [float(c) for c in np.polyfit(_xx, np.log(_xx), DEG)]

NX = 8
NI = 16
NPW = 8

NK = 100
SCRATCH = {
    "xb": ("sbuf", [128, 512], "bfloat16"),
    "wb": ("sbuf", [128, 768], "bfloat16"),
    "xq": ("sbuf", [128, 128], "float8_e4m3fn_x4"),
    "xs": ("sbuf", [128, 128], "uint8"),
    "fq": ("sbuf", [128, 128], "float8_e4m3fn_x4"),
    "fs": ("sbuf", [128, 128], "uint8"),
    "wq": ("sbuf", [128, 3 * NC], "float8_e4m3fn_x4"),
    "ws": ("sbuf", [128, 3 * NC], "uint8"),
    "lq": ("sbuf", [128, 2 * NC], "float8_e4m3fn_x4"),
    "lz": ("sbuf", [128, 2 * NC], "uint8"),
    "cid": ("sbuf", [128, NC], "float32"),
    "mk": ("sbuf", [128, 6 * NC], "float32"),
    "pr": ("sbuf", [128, 6 * NC + 8], "float32"),
    "ex": ("sbuf", [128, 6 * NC], "float32"),
    "dm": ("sbuf", [128, 6 * NC + 8], "float32"),
    "ps": ("psum", [128, 6 * BANK], "float32"),
    "tgd": ("dram", [128, 2], "bfloat16"),
}
for _n in ("tgo", "tgf"):
    SCRATCH[_n] = ("sbuf", [128, 16], "bfloat16")
for _n in ("ix1", "ix2", "mx", "nb1", "nb2", "nb3", "sa", "st1", "rb", "rt", "yt", "tt", "mm", "ww", "pa", "ub", "us", "xv", "hs",
           "gg", "nn", "zb", "on", "cf"):
    SCRATCH[_n] = ("sbuf", [128, 8], "float32")
for _n in ("lt", "zz", "lk", "thr", "hv", "ck", "vb", "fe"):
    SCRATCH[_n] = ("sbuf", [128, 16], "float32")
_REM = ["tgf", "xc", "xs", "wcP", "wsP"] + [a + b for a in ("wc", "ws", "lc", "lz") for b in "AB"] + ["rb", "rt", "ls"]
SEMAPHORES = _REM + ["k%d" % i for i in range(NK)]
SLOT = {"A": 0, "P": 1, "B": 2}
LATE = {"A": (0, NC), "B": (NC, 2 * NC)}


def plan(T, topo):
    chips = sorted({topo.chip(c) for c in T.cores})
    out = {}
    for ch in chips:
        here = [c for c in T.cores if topo.chip(c) == ch]
        there = [c for c in T.cores if topo.chip(c) != ch]
        P = [c for c in here if all(topo.may_write(c, d) for d in there)][0]
        A, B = sorted([c for c in here if c != P], key=lambda c: topo.die(c) != topo.die(P))
        helpers = [c for c in range(SIM_CORES) if topo.chip(c) == ch and T.rank_of(c) is None and all(topo.may_write(c, d) for d in there)]
        hB = sorted(helpers, key=lambda c: topo.die(c) != topo.die(B))[:2]
        hA = [c for c in helpers if c not in hB][0]
        out[ch] = {"P": P, "A": A, "B": B, "relA": [P, hA], "relB": hB}
    return chips, out


def rank_program(g, core, T, topo):
    chips, plans = plan(T, topo)
    ch = topo.chip(core)
    me = plans[ch]
    ot = plans[[c for c in chips if c != ch][0]]
    mates = [ot["A"], ot["B"]]
    Q = {"g": g, "v": g.vector, "t": g.tensor, "s": g.scalar, "y": g.sync}
    seen, made, sent = set(), [], [0]

    def need(q, *keys):
        for k in keys:
            if (q, k) not in seen:
                seen.add((q, k))
                Q[q].wait_ge(T.sem[k[0]], k[1])

    def done(inst, n=1):
        key = ("k%d" % len(made), n)
        made.append(key)
        inst.then_inc(T.sem[key[0]], n)
        return key

    def engines(dst, lo, n):
        m = topo.mask(core, dst)
        bits = [i for i in range(m.bit_length()) if (m >> i) & 1]
        return sum(1 << i for i in bits[lo:lo + n])

    def count(mask):
        return bin(mask).count("1")

    def send(dst, out, in_, sem, mask):
        a = topo.addr(dst)
        g.remote_dma(out, in_, T.sem[sem], T.sem.ls, a[1], a[0], mask)
        sent[0] += count(mask)

    def fused(*items):
        trs = []
        for dsts, out, in_, sem, mask in items:
            ids = [DstId(rid=topo.addr(d)[0], pnc=topo.addr(d)[1]) for d in dsts]
            trs.append(RemoteDMATransfer(dst_ids=ids, dma_engine_mask=mask, remote_sem=T.sem[sem], srcs=[in_], dsts=[out for _ in dsts]))
            sent[0] += count(mask)
        g.remote_dma_fused(trs, local_sem=T.sem.ls)

    def u8(v):
        return v.bitcast(dt.uint8)

    def W(r):
        lo = SLOT[r] * NC
        return T.wq[:, lo:lo + NC], T.ws[:, lo:lo + NC]

    def relay(r):
        lo, hi = LATE[r]
        q, z = W(r)
        rel = me["rel" + r]
        dst = mates[rel.index(core)]
        m = engines(dst, 0, NX)
        if core != me["P"]:
            need("g", ("ws" + r, NI))
            send(dst, T.lz[:, lo:hi], z, "lz" + r, m)
        need("g", ("wc" + r, NI))
        send(dst, u8(T.lq[:, lo:hi]), u8(q), "lc" + r, m)
        if core != me["P"] and me["P"] in rel:
            send(mates[rel.index(me["P"])], T.lz[:, lo:hi], z, "lz" + r, m)

    role = [r for r in "PAB" if me[r] == core]
    if not role:
        for r in "AB":
            if core in me["rel" + r]:
                relay(r)
                need("g", ("ls", sent[0]))
        return
    role = role[0]
    v, s, t, y = g.vector, g.scalar, g.tensor, g.sync
    wq, ws = W(role)

    ktd = done(s.dma_start(T.tgd[:, :], T.tg[:, :]), 16)
    K = {}
    for n in ("xw" if role == "P" else "wx"):
        K[n] = done(y.dma_start(T[n + "b"][:, :], T[n][:, :]), 16)
    ktg = done(s.dma_start(T.tgo[:, 0:2], T.tg[:, :]), 16)
    kio = done(g.iota(T.cid[:, :], [[1, NC]], 0, 0, allow_small_or_imprecise_dtypes=True))

    k0 = done(v.memset(T.lt[:, 0:KP], LN2))
    kzz = done(v.memset(T.zz[:, 0:KP], 0.0))
    need("v", k0, kzz)
    klk = done(v.tensor_tensor_scan(T.lk[:, 0:KP], T.lt[:, 0:KP], T.zz[:, 0:KP], 0.0, OP.add, OP.add))
    need("s", klk)
    kthr = done(s.activation(T.thr[:, 0:KP], T.lk[:, 0:KP], AF.Exp))

    def quant(n, q, z):
        need("v", K[n])
        return done(v.quantize_mx(q, z, T[n + "b"][:, :]))

    if role == "P":
        kqx = quant("x", T.xq[:, :], T.xs[:, :])
    kqw = quant("w", wq, ws)
    if role != "P":
        kqx = quant("x", T.xq[:, :], T.xs[:, :])

    need("g", ktd)
    if role == "P":
        other, B2, A1 = ot["P"], ot["B"], me["A"]
        m = engines(other, 0, NX)
        mi = engines(A1, NX, NPW)
        send(other, T.tgf[:, 0:2], T.tgd[:, :], "tgf", m)
        need("g", kqx)
        send(other, u8(T.fq[:, :]), u8(T.xq[:, :]), "xc", m)
        send(other, T.fs[:, :], T.xs[:, :], "xs", m)
        need("g", kqw)
        fused(([B2], u8(wq), u8(wq), "wcP", m), ([A1], u8(wq), u8(wq), "wcP", mi))
        fused(([B2], ws, ws, "wsP", m), ([A1], ws, ws, "wsP", mi))
        for r in "AB":
            if core in me["rel" + r]:
                relay(r)
        nf, nwp = NX, None
    else:
        other = me["B" if role == "A" else "A"]
        rel = me["rel" + role]
        m = engines(other, 0, NI)
        send(other, T.tgf[:, 0:2], T.tgd[:, :], "tgf", m)
        need("g", kqw)
        fused((rel, ws, ws, "ws" + role, m))
        fused((rel, u8(wq), u8(wq), "wc" + role, m))
        need("g", kqx)
        send(other, u8(T.fq[:, :]), u8(T.xq[:, :]), "xc", m)
        send(other, T.fs[:, :], T.xs[:, :], "xs", m)
        if me["P"] not in rel:
            send(me["P"], u8(wq), u8(wq), "wc" + role, m)
            send(me["P"], ws, ws, "ws" + role, m)
        nf, nwp = NI, (NPW if role == "A" else NX)

    own, far = (T.xq[:, :], T.xs[:, :], [kqx]), (T.fq[:, :], T.fs[:, :], [("xc", nf), ("xs", nf)])
    B = []

    def block(X, r, late=False):
        if late:
            lo, hi = LATE[r]
            B.append((X, T.lq[:, lo:hi], T.lz[:, lo:hi], [("lz" + r, NX), ("lc" + r, NX)], T.rank_of(ot[r])))
        else:
            q, z = W(r)
            if r == role:
                ks = [kqw]
            else:
                n = nwp if r == "P" else NI
                ks = [("wc" + r, n), ("ws" + r, n)]
            B.append((X, q, z, ks, T.rank_of((ot if r == "P" and role == "B" else me)[r])))

    if role == "P":
        SET = {1: (0, 3), 2: (3, 6)}
        for X in (far, own):
            for r in "PAB":
                block(X, r)
        gaps = (2, 5)
    else:
        SET = {1: (0, 2), 2: (2, 4), 3: (4, 6)}
        for X in (far, own):
            block(X, role)
            block(X, "P")
        block(own, "A", True)
        block(own, "B", True)
        gaps = (1, 3, 4)
    at = [NC * i + sum(1 for j in gaps if j <= i) for i in range(6)]
    after = set()
    D = {}

    def bank(i):
        return T.ps[:, BANK * i:BANK * i + NC]

    def index(k):
        ix, tg = T["ix%d" % k], (T.tgf if k == 1 else T.tgo)
        need("v", ("tgf", nf) if k == 1 else ktg)
        D["ix%d" % k] = done(v.tensor_scalar(ix[:, 0:1], tg[:, 0:1], float(NC), tg[:, 1:2], OP.mult, OP.add))

    def mask(k, i):
        need("v", kio, D["ix%d" % k])
        D["m%d" % i] = done(v.tensor_scalar(T.mk[:, NC * i:NC * (i + 1)], T.cid[:, :], T["ix%d" % k][:, 0:1], -float(NC * B[i][4]), OP.subtract, OP.is_equal))

    def product(i):
        X, q, z, ks, _ = B[i]
        need("t", *X[2])
        need("t", *ks)
        D["p%d" % i] = done(t.matmul_mx(bank(i), X[0], X[1], q, z, True, True))

    def top(i):
        need("v", D["p%d" % i])
        D["x%d" % i] = done(v.tensor_reduce(T.mx[:, i:i + 1], bank(i), AxisListType.X, OP.max))

    def pick(i):
        need("v", D["m%d" % i], D["p%d" % i])
        if i in after:
            need("v", D["e%d" % i])
        D["k%d" % i] = done(v.tensor_tensor(T.pr[:, at[i]:at[i] + NC], bank(i), T.mk[:, NC * i:NC * (i + 1)], OP.mult))

    def expo(i, k):
        need("s", D["nb%d" % k], D["k%d" % i] if i not in after else D["x%d" % i])
        D["e%d" % i] = done(s.activation(T.ex[:, NC * i:NC * (i + 1)], bank(i), AF.Exp, bias=T["nb%d" % k][:, 0:1], scale=SCALE, accum_out=T.sa[:, i:i + 1]))

    def gather(lo, hi, name, *keys, out=None):
        a, b = at[lo] - (1 if keys else 0), at[hi - 1] + NC
        need("s", *keys)
        need("s", *[D["k%d" % i] for i in range(lo, hi)])
        if out is None:
            D[name] = done(s.activation(T.dm[:, a:b], T.pr[:, a:b], AF.Identity, accum_out=T.pr[:, at[hi] - 1:at[hi]]))
        else:
            D[name] = done(s.activation(T.dm[:, a:b], T.pr[:, a:b], AF.Identity, scale=SCALE, accum_out=out))

    def shift(k, st, o):
        lo, hi = SET[k]
        nb = T["nb%d" % k]
        need("v", *[D["x%d" % i] for i in range(lo, hi)])
        if hi - lo == 2:
            D["nb%d" % k] = done(v.tensor_scalar(nb[:, 0:1], T.mx[:, lo:lo + 1], T.mx[:, lo + 1:lo + 2], -SCALE, OP.max, OP.mult))
            D["c%d" % k] = done(v.tensor_tensor(st[:, o:o + 1], T.mx[:, lo:lo + 1], T.mx[:, lo + 1:lo + 2], OP.max))
        else:
            D["c%d" % k] = done(v.tensor_scalar(st[:, o:o + 1], T.mx[:, lo:lo + 1], T.mx[:, lo + 1:lo + 2], T.mx[:, lo + 2:lo + 3], OP.max, OP.max))
            need("v", D["c%d" % k])
            D["nb%d" % k] = done(v.tensor_scalar(nb[:, 0:1], st[:, o:o + 1], -SCALE, None, OP.mult))

    def total(k, st, o):
        lo, hi = SET[k]
        need("v", *[D["e%d" % i] for i in range(lo, hi)])
        if hi - lo == 2:
            D["s%d" % k] = done(v.tensor_tensor(st[:, o + 1:o + 2], T.sa[:, lo:lo + 1], T.sa[:, lo + 1:lo + 2], OP.add))
        else:
            D["s%d" % k] = done(v.tensor_scalar(st[:, o + 1:o + 2], T.sa[:, lo:lo + 1], T.sa[:, lo + 1:lo + 2], T.sa[:, lo + 2:lo + 3], OP.add, OP.add))

    def share():
        need("g", D["c1"], D["s1"])
        send(other, T.rb[:, 0:2], T.st1[:, 0:2], "rb", m)
        need("g", D["t1"])
        send(other, T.rt[:, 0:1], T.tt[:, 0:1], "rt", m)

    def tables():
        kh0 = done(v.memset(T.hv[:, 0:KP], 0.5))
        ks = [done(v.memset(T.on[:, 0:ND], 1.0))]
        need("v", kh0)
        kc = done(v.tensor_tensor_scan(T.ck[:, 0:KP], T.hv[:, 0:KP], T.zz[:, 0:KP], 0.5, OP.mult, OP.add))
        need("v", kc)
        ks.append(done(v.memset(T.ck[:, KP - 1:KP], 2.0 ** -KP)))
        for j, c in enumerate(POLY):
            ks.append(done(v.memset(T.cf[:, j:j + 1], c)))
        return ks

    def weights():
        need("s", ("rb", nf), D["c2"], D["nb3"])
        D["w"] = done(s.activation(T.ww[:, 0:2], T.rb[:, 0:8:4], AF.Exp, bias=T.nb3[:, 0:1], scale=SCALE))

    def early():
        need("v", D["w"], D["s2"])
        kpa = done(v.tensor_tensor(T.pa[:, 0:2], T.ww[:, 0:2], T.rb[:, 1:8:4], OP.mult))
        need("v", kpa, *ktab)
        D["ub"] = done(v.tensor_scalar(T.ub[:, 0:ND], T.on[:, 0:ND], T.pa[:, 0:1], T.pa[:, 1:2], OP.mult, OP.add))

    def base():
        need("v", D["nb3"])
        D["zb"] = done(v.tensor_scalar(T.zb[:, 0:1], T.nb3[:, 0:1], -1.0, KP * LN2, OP.mult, OP.add))

    def finish(u, ku, add, kt):
        ks = [ku, kthr] + ([] if add is None else [add[1]])
        need("v", *ks)
        if add is None:
            kvb = done(v.tensor_scalar(T.vb[:, 0:KP], T.thr[:, 0:KP], u[:, 0:1], None, OP.is_gt))
        else:
            kvb = done(v.tensor_scalar(T.vb[:, 0:KP], T.thr[:, 0:KP], add[0], u[:, 0:1], OP.subtract, OP.is_gt))
        need("v", kvb)
        kfe = done(v.tensor_tensor_scan(T.fe[:, 0:KP], T.vb[:, 0:KP], T.ck[:, 0:KP], 0.5, OP.mult, OP.add))
        knn = done(v.tensor_reduce(T.nn[:, 0:1], T.vb[:, 0:KP], AxisListType.X, OP.add))
        need("v", kfe)
        if add is None:
            kxv = done(v.tensor_scalar(T.xv[:, 0:ND], u[:, 0:ND], T.fe[:, KP - 1:KP], None, OP.mult))
        else:
            kxv = done(v.tensor_scalar(T.xv[:, 0:ND], u[:, 0:ND], add[0], T.fe[:, KP - 1:KP], OP.add, OP.mult))
        need("v", knn, D["zb"])
        kg1 = done(v.tensor_scalar(T.gg[:, 1:2], T.nn[:, 0:1], -LN2, T.zb[:, 0:1], OP.mult, OP.add))
        need("v", kxv)
        khs = done(v.tensor_tensor_scan(T.hs[:, 0:ND], T.xv[:, 0:ND], T.cf[:, 0:ND], 0.0, OP.mult, OP.add))
        need("v", kg1, kt, ("rt", nf))
        kg0 = done(v.tensor_scalar(T.gg[:, 0:1], T.gg[:, 1:2], T.tt[:, 1:2], T.rt[:, 0:1], OP.subtract, OP.subtract))
        need("v", khs, kg0)
        return done(v.tensor_scalar(T.yt[:, 0:2], T.gg[:, 0:2], T.hs[:, ND - 1:ND], None, OP.add))

    index(2)
    for i in range(*SET[2]):
        mask(2, i)
    if role == "P":
        for i in (3, 4, 0, 1, 5, 2):
            product(i)
        top(3)
        pick(3)
        ktab = tables()
        index(1)
        for i in (0, 1, 2):
            mask(1, i)
        top(4)
        pick(4)
        gather(3, 5, "g2")
        top(0)
        pick(0)
        top(1)
        pick(1)
        gather(0, 2, "g1")
        top(2)
        shift(1, T.st1, 0)
        pick(2)
        for i in (0, 1, 2):
            expo(i, 1)
        top(5)
        shift(2, T.rb, 4)
        total(1, T.st1, 0)
        pick(5)
        gather(2, 3, "t1", D["g1"], out=T.tt[:, 0:1])
        share()
        for i in (3, 4, 5):
            expo(i, 2)
        gather(5, 6, "t2", D["g2"], out=T.tt[:, 1:2])
        total(2, T.rb, 4)
        need("v", D["c2"], ("rb", nf))
        D["nb3"] = done(v.tensor_scalar(T.nb3[:, 0:1], T.rb[:, 0:1], T.rb[:, 4:5], -SCALE, OP.max, OP.mult))
        weights()
        base()
        early()
        ky = finish(T.ub, D["ub"], None, D["t2"])
    else:
        for i in (2, 0, 1, 3, 4, 5):
            product(i)
        mask(2, 4)
        mask(2, 5)
        ktab = tables()
        top(2)
        pick(2)
        gather(2, 3, "g2")
        index(1)
        mask(1, 0)
        mask(1, 1)
        top(0)
        pick(0)
        gather(0, 1, "g1")
        top(1)
        shift(1, T.st1, 0)
        pick(1)
        expo(0, 1)
        expo(1, 1)
        gather(1, 2, "t1", D["g1"], out=T.tt[:, 0:1])
        top(3)
        shift(2, T.rb, 4)
        total(1, T.st1, 0)
        pick(3)
        share()
        expo(2, 2)
        expo(3, 2)
        gather(3, 4, "g3", D["g2"])
        top(4)
        total(2, T.rb, 4)
        need("v", D["x4"], D["c2"], ("rb", nf))
        km = done(v.tensor_scalar(T.mm[:, 0:1], T.mx[:, 4:5], T.rb[:, 0:1], T.rb[:, 4:5], OP.max, OP.max))
        top(5)
        need("v", km, D["x5"])
        D["nb3"] = done(v.tensor_scalar(T.nb3[:, 0:1], T.mx[:, 5:6], T.mm[:, 0:1], -SCALE, OP.max, OP.mult))
        pick(5)
        after.add(4)
        weights()
        expo(4, 3)
        expo(5, 3)
        early()
        pick(4)
        gather(4, 6, "t3", D["g3"], out=T.tt[:, 1:2])
        need("v", D["ub"], D["e4"])
        kus = done(v.tensor_scalar(T.us[:, 0:ND], T.ub[:, 0:ND], T.sa[:, 4:5], None, OP.add))
        base()
        ky = finish(T.us, kus, (T.sa[:, 5:6], D["e5"]), D["t3"])
    need("y", ky)
    kyo = done(y.dma_start(T.y[:, :], T.yt[:, 0:2]), 16)
    need("y", kyo)

    need("g", ("ls", sent[0]))
    waited = {k for _, k in seen}
    need("g", *[k for k in made if k not in waited])
